import numpy as np, ml_dtypes
CORES = [40,64,80,88,96,104,120,144]
N = 8
import mx_ref
BF = ml_dtypes.bfloat16
def entries(a):
    return np.ascontiguousarray(a.T).reshape(-1)
def table(e):
    return np.ascontiguousarray(np.reshape(e, (-1, 16)).T).astype(np.int32)
def f(rng, *shape):
    return mx_ref.flush((rng.standard_normal(shape, dtype=np.float32) * np.exp2(rng.integers(-2, 3, shape[:-1] + (1,)))).astype(BF))
def wide(rng, *shape, cols=0):
    v = rng.standard_normal(shape, dtype=np.float32) * np.exp2(rng.integers(-12, 13, shape)).astype(np.float32)
    if cols: v *= np.repeat(np.exp2(rng.integers(-cols, cols + 1, shape[:-2] + (1, shape[-1] // 4))) * (rng.random(shape[:-2] + (1, shape[-1] // 4)) > 0.0625), 4, axis=-1).astype(np.float32)
    return mx_ref.flush(v.astype(BF))
T, ND, CD, LM, CAPP = 512, 64, 16, 64, 128
def lens(rng, n, total):
    a = 1 + np.minimum(LM - 1, rng.multinomial(total - n, rng.dirichlet(np.ones(n))))
    for i in rng.permutation(n): a[i] += min(LM - a[i], total - a.sum())
    return a
def places(rng, l):
    o = rng.permutation(ND); g = rng.multinomial(T - l.sum(), rng.dirichlet(np.ones(ND + 1)))
    s = np.zeros(ND, int); s[o] = np.cumsum(g[:ND]) + np.cumsum(l[o]) - l[o]
    return s
def pick(rng, l):
    p = rng.permutation(ND); a, b = p[:CD].copy(), p[CD:].copy()
    while l[a].sum() > CAPP:
        i = np.argmax(l[a]); j = rng.choice(np.flatnonzero(l[b] < l[a[i]]))
        a[i], b[j] = b[j], a[i]
    return rng.permutation(a)
def lists(rng, kind="any"):
    s, n, c = [], [], np.zeros((N, N * CD), int)
    K, J = (T - ND) // (LM - 1), (CAPP - CD) // (LM - 1)
    TT = min(T, ND // CD * CAPP)
    for q in range(N):
        d = rng.permutation(ND); l = np.ones(ND, int)
        if kind == "long": l[d[:K]] = LM
        elif kind == "full": l[d] = np.concatenate([lens(rng, CD, CAPP), lens(rng, CD, CAPP), lens(rng, ND - 2 * CD, T - 2 * CAPP)])
        elif kind == "any": l[d] = lens(rng, ND, int(rng.integers(TT - TT // 4, TT + 1)))
        s.append(table(places(rng, l))); n.append(table(l))
        for r in range(N):
            if kind == "long": e = rng.permutation(np.concatenate([rng.permutation(d[:K])[:J], rng.permutation(d[K:])[:CD - J]]))
            elif kind == "full": k = CD * int(rng.integers(0, 2)); e = rng.permutation(d[k:k + CD])
            else: e = pick(rng, l)
            c[r, CD * q:CD * q + CD] = e
    return {"st": np.stack(s), "ln": np.stack(n), "cd": np.stack([table(c[r]) for r in range(N)])}
def setup_inputs(rng):
    return {"x": f(rng, N, 128, 4 * T), "qw": f(rng, N, 128, 512), **lists(rng)}
def setup_inputs_long(rng):
    return {**setup_inputs(rng), **lists(rng, "long")}
def setup_inputs_ones(rng):
    return {**setup_inputs(rng), **lists(rng, "ones")}
def setup_inputs_full(rng):
    return {**setup_inputs(rng), **lists(rng, "full")}
def setup_inputs_below(rng):
    d = setup_inputs(rng); p = rng.permutation(N)
    s, u = rng.integers(-20, 27, N), rng.integers(-20, 28, N)
    s[p[0]] = 26; u[rng.choice(p[:-1])] = 27; s[p[-1]] = 0; u[p[-1]] = 0
    d["x"] = mx_ref.flush((-np.exp2(rng.uniform(-3, 3, (N, 128, 4 * T)) + s[:, None, None])).astype(BF))
    d["qw"] = mx_ref.flush(np.exp2(rng.uniform(-2, 2, (N, 128, 512)) + u[:, None, None]).astype(BF))
    return d
def setup_inputs_spread(rng):
    d = setup_inputs(rng); d["x"] = wide(rng, N, 128, 4 * T, cols=8); return d
def check_inputs(d):
    b = []
    L = [entries(d["ln"][r]).astype(np.int64) for r in range(N)]
    for r in range(N):
        s, l = entries(d["st"][r]).astype(np.int64), L[r]
        if l.min() < 1 or l.max() > LM: b.append("ln")
        o = np.argsort(s, kind="stable")
        if s.min() < 0 or (s + l).max() > T or (s[o][:-1] + l[o][:-1] > s[o][1:]).any(): b.append("st")
        c = entries(d["cd"][r])
        if c.min() < 0 or c.max() >= ND: b.append("cd"); continue
        for q in range(N):
            e = c[CD * q:CD * q + CD]
            if len(set(e.tolist())) != CD or L[q][e].sum() > CAPP: b.append("cd")
    return sorted(set(b))
def reference(x, qw, st, ln, cd):
    X = [mx_ref.quantize(x[q]) for q in range(N)]
    y = np.zeros((N, 128, N * CD), np.float32)
    for r in range(N):
        W = mx_ref.quantize(qw[r]); c = entries(cd[r])
        for q in range(N):
            z = mx_ref.matmul(W, X[q]); s, l = entries(st[q]), entries(ln[q])
            for i in range(CD * q, CD * q + CD):
                y[r][:, i] = z[:, s[c[i]]:s[c[i]] + l[c[i]]].max(axis=1)
    return {"y": y}

@@ -1,0 +1,445 @@
+from concourse.bass import DstId, RemoteDMATransfer
+from concourse.mybir import dt, AluOpType as A, ActivationFunctionType as F
+
+N, TOK, CAP = 8, 512, 128
+BIG, FAR, LIFT = 1.0e29, 1.0e6, 4096.0
+WB = 136
+VB = {"S": 0, "O": 408, "M": 952}
+GB = {"S": 0, "O": 56, "M": 128}
+EB = {"S": 0, "O": 4, "M": 8}
+PB = {"S": 0, "O": 3, "M": 7}
+CARRY = {0: (0, 3), 1: (1, 2)}
+
+SCRATCH = {
+    "cdi": ("sbuf", [128, 8], "int32"), "cdu": ("sbuf", [128, 8], "uint16"), "cdm": ("sbuf", [128, 2], "uint16"),
+    "row": ("sbuf", [1, 128], "int32"), "tab": ("sbuf", [128, 128], "int32"),
+    "stt": ("sbuf", [128, 64], "float32"), "lnt": ("sbuf", [128, 64], "float32"),
+    "nes": ("sbuf", [128, 64], "float32"), "nen": ("sbuf", [128, 64], "float32"),
+    "poi": ("sbuf", [128, 4], "int32"), "poa": ("sbuf", [128, 4], "int32"), "pou": ("sbuf", [128, 4], "uint16"),
+    "pp": ("sbuf", [128, 1], "int32"), "ki": ("sbuf", [128, 3], "int32"), "kf": ("sbuf", [128, 3], "float32"),
+    "csu": ("sbuf", [128, 1], "float32"), "cst": ("sbuf", [128, 1], "float32"), "zz": ("sbuf", [128, 1032], "bfloat16"),
+    "ii": ("sbuf", [128, 64], "float32"), "jj": ("sbuf", [128, 128], "float32"),
+    "le": ("sbuf", [128, 64], "float32"), "dmb": ("sbuf", [128, 128], "float32"), "dmk": ("sbuf", [128, 128], "float32"),
+    "rst": ("sbuf", [128, 64], "float32"), "fr": ("sbuf", [128, 128], "float32"), "neg": ("sbuf", [128, 64], "float32"),
+    "cds": ("sbuf", [128, 4], "uint16"), "cdo": ("sbuf", [128, 4], "uint16"),
+    "g1": ("sbuf", [128, 152], "float32"), "s1": ("sbuf", [128, 152], "float32"), "g2": ("sbuf", [128, 152], "float32"),
+    "dl": ("sbuf", [128, 152], "float32"), "en0": ("sbuf", [128, 16], "uint16"),
+    "vv": ("sbuf", [128, 1088], "float32"),
+    "la": ("sbuf", [128, 1024], "float32"), "lb": ("sbuf", [128, 1024], "float32"),
+    "off": ("sbuf", [128, 256], "uint16"),
+    "xs": ("sbuf", [128, 4 * (TOK + CAP)], "bfloat16"), "ws": ("sbuf", [128, 512], "bfloat16"),
+    "tile": ("sbuf", [128, 4096], "bfloat16"),
+    "qc": ("sbuf", [128, 1024], "float8_e4m3fn_x4"), "qp": ("sbuf", [128, 1024], "uint8"),
+    "wc": ("sbuf", [128, 128], "float8_e4m3fn_x4"), "wp": ("sbuf", [128, 128], "uint8"),
+    "lc": ("sbuf", [128, 896], "float8_e4m3fn_x4"), "lp": ("sbuf", [128, 896], "uint8"),
+    "el": ("sbuf", [128, 8], "float32"), "ef": ("sbuf", [128, 12], "float32"), "en": ("sbuf", [128, 12], "uint16"),
+    "mk": ("sbuf", [128, 1032], "float32"), "so": ("sbuf", [128, 1024], "float32"), "ys": ("sbuf", [128, 128], "float32"),
+    "ps": ("psum", [128, 4096], "float32"),
+    "hcd": ("sbuf", [128, 8], "uint16"), "hen": ("sbuf", [128, 1], "float32"),
+    "hc": ("sbuf", [128, 128], "float8_e4m3fn_x4"), "hp": ("sbuf", [128, 256], "uint8"),
+}
+SEMAPHORES = (["vec", "act", "pe", "gc", "lcd", "ltab", "lx", "lw", "ly", "sent", "cds", "cdo", "ens", "eno",
+               "hcd", "hen", "hc", "hp", "hq"] + ["t%d" % s for s in range(7)])
+
+
+def groups(T, topo, r):
+    own = [q for q in range(N) if q == r or topo.may_write(T.cores[r], T.cores[q])]
+    oth = [q for q in range(N) if q not in own]
+    a = own.index(r)
+    return [own[(a + j) % len(own)] for j in range(len(own))], [oth[(a + k) % len(oth)] for k in range(len(oth))], a
+
+
+def helpers(T, topo, r):
+    c = T.cores[r]
+    dst = T.cores[groups(T, topo, r)[1][0]]
+    hs = [h for h in topo.cores_of(c) if h != c and topo.may_write(h, dst)]
+    near = [h for h in hs if topo.die(h) == topo.die(c)]
+    far = [h for h in hs if topo.die(h) != topo.die(c)]
+    return [near[0], far[0], near[1], far[1]]
+
+
+def part(e, i, n):
+    w = len(e) // n
+    return e[i * w:(i + 1) * w]
+
+
+def bits(e):
+    return sum(1 << x for x in e)
+
+
+def upper(topo, c, h):
+    e = topo.engines(c, h)
+    return e[len(e) // 2:]
+
+
+def lists_up(topo, c, h, k):
+    return part(upper(topo, c, h), k, 2)
+
+
+def ends_up(topo, c, h, k):
+    return part(upper(topo, c, h), k, 4)
+
+
+def codes_up(topo, c, h, k):
+    return part(upper(topo, c, h), k, 2) if k in CARRY else part(topo.engines(c, h), k - 2, 2)
+
+
+def plane_up(topo, c, h, k):
+    return part(topo.engines(c, h), k, 4) if k in CARRY else part(topo.engines(c, h), k - 2, 2)
+
+
+def lane_same(topo, c, d, j):
+    return part(topo.engines(c, d), j - 1, 4)
+
+
+def codes_same(topo, c, d, j):
+    e = topo.engines(c, d)
+    return part(e, j - 1, 2) if j < 3 else e
+
+
+def plane_same(topo, c, d, j):
+    e = topo.engines(c, d)
+    return part(e, j - 1, 4) if j < 3 else part(e, 1, 2)
+
+
+def u8(ap):
+    return ap.bitcast(dt.uint8)
+
+
+def hand_on(g, core, T, topo, r, k):
+    _, oth, a = groups(T, topo, r)
+    rc = T.cores[r]
+    sent = [0]
+
+    def slot(n):
+        return (a - groups(T, topo, oth[n])[2]) % 4
+
+    def to(n):
+        return T.cores[oth[n]]
+
+    def on(n, dst, src, sem, eng):
+        rid, pid = topo.addr(to(n), core)
+        g.remote_dma(dst, src, T.sem[sem], T.sem.sent, pid, rid, bits(eng))
+        sent[0] += len(eng)
+
+    if k in CARRY:
+        g.wait_ge(T.sem.hcd, len(lists_up(topo, rc, core, k)))
+        ts = []
+        for i, n in enumerate(CARRY[k]):
+            rid, pid = topo.addr(to(n), core)
+            e = part(topo.engines(core, to(n)), i, 2)
+            ts.append(RemoteDMATransfer(dst_ids=[DstId(rid=rid, pnc=pid)], dma_engine_mask=bits(e), remote_sem=T.sem.cdo,
+                                        src=T.hcd[:, oth[n]:oth[n] + 1], dst=T.cdo[:, slot(n):slot(n) + 1]))
+            sent[0] += len(e)
+        g.remote_dma_fused(ts, local_sem=T.sem.sent)
+    e = topo.engines(core, to(k))
+    g.wait_ge(T.sem.hen, len(ends_up(topo, rc, core, k)))
+    on(k, T.el[:, 3 + slot(k):4 + slot(k)], T.hen[:, 0:1], "eno", e)
+    s = 3 + slot(k)
+    g.wait_ge(T.sem.hc, len(codes_up(topo, rc, core, k)))
+    on(k, u8(T.lc[:, 128 * s:128 * s + 128]), u8(T.hc[:, 0:128]), "t%d" % s, e)
+    if k in CARRY:
+        for i, n in enumerate(CARRY[k]):
+            s = 3 + slot(n)
+            g.wait_ge(T.sem["hp" if i == 0 else "hq"], len(plane_up(topo, rc, core, n)))
+            on(n, T.lp[:, 128 * s:128 * s + 128], T.hp[:, 128 * i:128 * i + 128], "t%d" % s, topo.engines(core, to(n)))
+    g.wait_ge(T.sem.sent, sent[0])
+
+
+def rank_program(g, core, T, topo):
+    rank = T.rank_of(core)
+    if rank is None:
+        for r in range(N):
+            if T.cores[r] in topo.cores_of(core):
+                hs = helpers(T, topo, r)
+                if core in hs:
+                    hand_on(g, core, T, topo, r, hs.index(core))
+        return
+    own, oth, a = groups(T, topo, rank)
+    hs = helpers(T, topo, rank)
+    v, sc, pe = g.vector, g.scalar, g.tensor
+    queue = {"v": v, "s": sc, "t": pe, "g": g, "y": g.sync}
+    cnt = {"vec": 0, "act": 0, "pe": 0, "gc": 0, "sent": 0}
+    seen = {}
+
+    def need(q, sem, val):
+        if seen.get((q, sem), 0) < val:
+            queue[q].wait_ge(T.sem[sem], int(val))
+            seen[(q, sem)] = val
+
+    def done(sem, ins):
+        cnt[sem] += 1
+        ins.then_inc(T.sem[sem], 1)
+        return cnt[sem]
+
+    def V(ins):
+        return done("vec", ins)
+
+    def S(ins):
+        return done("act", ins)
+
+    for i in range(8):
+        (g.sync if i % 2 == 0 else sc).dma_start(T.cdi[16 * i:16 * i + 16, :], T.cd[:]).then_inc(T.sem.lcd, 16)
+    g.sync.dma_start(T.row[0:1, 0:64], T.st[:]).then_inc(T.sem.ltab, 16)
+    sc.dma_start(T.row[0:1, 64:128], T.ln[:]).then_inc(T.sem.ltab, 16)
+    g.sync.dma_start(T.xs[:, 0:4 * TOK], T.x[:]).then_inc(T.sem.lx, 16)
+    sc.dma_start(T.ws[:], T.qw[:]).then_inc(T.sem.lw, 16)
+
+    done("gc", g.iota(T.pp[:], [[0, 1]], 0, 1))
+    i_io = done("gc", g.iota(T.poi[:], [[1, 4]], 0, 4))
+    done("gc", g.iota(T.ii[:], [[0, 4], [1, 16]], 0, 0, allow_small_or_imprecise_dtypes=True))
+    done("gc", g.iota(T.jj[:], [[0, 32], [1, 4]], 0, 0, allow_small_or_imprecise_dtypes=True))
+
+    i_z = V(v.memset(T.zz[:], 0.0))
+    need("s", "vec", i_z)
+    i_vv = {}
+    for bt, R in (("S", 3), ("O", 4), ("M", 1)):
+        i_vv[bt] = S(sc.activation(T.vv[:, VB[bt]:VB[bt] + WB * R], T.zz[:, 0:WB * R], F.Copy))
+    i_fr = S(sc.activation(T.fr[:], T.zz[:, 0:128], F.Copy, bias=4.0))
+    S(sc.activation(T.neg[:], T.zz[:, 0:64], F.Copy, bias=-BIG))
+    i_mk = S(sc.activation(T.mk[:], T.zz[:], F.Copy, bias=BIG))
+    need("v", "gc", i_io)
+    V(v.tensor_scalar(T.ki[:, 0:1], T.pp[:], 15, None, A.bitwise_and))
+    V(v.tensor_scalar(T.ki[:, 1:2], T.pp[:], 3, None, A.bitwise_and))
+    V(v.tensor_scalar(T.ki[:, 2:3], T.pp[:], 15, 2, A.bitwise_and, A.arith_shift_right))
+    i_p = V(v.tensor_scalar(T.poa[:], T.poi[:], 63, None, A.bitwise_and))
+
+    need("v", "lcd", 128)
+    i_cd = V(v.tensor_copy(T.cdu[:], T.cdi[:]))
+    need("g", "vec", i_cd)
+
+    def fused(trs):
+        ts = []
+        for dc, dst, src, sem, e in trs:
+            rid, pid = topo.addr(dc, core)
+            ts.append(RemoteDMATransfer(dst_ids=[DstId(rid=rid, pnc=pid)], dma_engine_mask=bits(e),
+                                        remote_sem=T.sem[sem], src=src, dst=dst))
+            cnt["sent"] += len(e)
+        g.remote_dma_fused(ts, local_sem=T.sem.sent)
+
+    def at(d):
+        return (a - groups(T, topo, d)[2]) % 4
+
+    fused([(T.cores[own[j]], T.cds[:, at(own[j]) - 1:at(own[j])], T.cdu[:, own[j]:own[j] + 1], "cds",
+            lane_same(topo, core, T.cores[own[j]], j)) for j in range(1, 4)])
+    fused([(hs[k], T.hcd[:, 0:8], T.cdu[:, 0:8], "hcd", lists_up(topo, core, hs[k], k)) for k in CARRY])
+    need("g", "ltab", 32)
+    i_tab = done("gc", g.partition_broadcast(T.tab[:], T.row[0:1, :], 128))
+
+    need("v", "vec", i_p)
+    V(v.tensor_copy(T.kf[:], T.ki[:]))
+    i_k = V(v.tensor_copy(T.pou[:], T.poa[:]))
+    i_r = V(v.memset(T.rst[:], 0.0))
+    need("v", "gc", 4)
+    need("v", "vec", i_k)
+    V(v.tensor_scalar(T.le[:], T.ii[:], T.kf[:, 0:1], None, A.is_le))
+    i_m = V(v.tensor_scalar(T.dmb[:], T.jj[:], T.kf[:, 2:3], FAR + LIFT, A.is_gt, A.mult))
+    i_c = V(v.tensor_scalar(T.csu[:], T.kf[:, 2:3], -3.0, LIFT, A.add, A.mult))
+    need("v", "vec", i_r)
+    for b in range(1, 4):
+        V(v.memset(T.rst[:, 16 * b:16 * b + 1], float(WB * b)))
+    need("v", "vec", i_m)
+    V(v.tensor_scalar(T.dmk[:], T.dmb[:], -FAR, None, A.add))
+    need("v", "vec", i_c)
+    V(v.tensor_scalar(T.cst[:], T.csu[:], T.kf[:, 1:2], -4.0, A.add, A.add))
+    V(v.memset(T.g2[:], 0.0))
+    V(v.memset(T.xs[:, 4 * TOK:], 0.0))
+    need("v", "gc", i_tab)
+    i_ln = V(v.tensor_copy(T.lnt[:], T.tab[:, 64:128].indirect(T.pou[:, 0:4])))
+    i_st = V(v.tensor_scalar(T.stt[:], T.tab[:, 0:64].indirect(T.pou[:, 0:4]), 4.0, None, A.mult))
+    need("v", "vec", i_ln)
+    i = V(v.tensor_scalar(T.nes[:], T.lnt[:], -4.0, None, A.mult))
+    need("v", "vec", i)
+    i_ne = V(v.tensor_tensor(T.nen[:], T.nes[:], T.stt[:], A.subtract))
+
+    def ends(bt, R, off, on_s, fill=None):
+        gb, eb, vb = GB[bt], EB[bt], VB[bt]
+        w = 16 * R
+        need("v", "vec", i_ne)
+        if on_s:
+            need("s", "vec", i_st)
+            st = ("act", S(sc.activation(T.g2[:, gb:gb + w], T.stt[:, 0:64].indirect(off), F.Copy)))
+        i = V(v.tensor_tensor(T.g1[:, gb:gb + w], T.lnt[:, 0:64].indirect(off), T.le[:, 0:w], A.mult))
+        if not on_s:
+            st = ("vec", V(v.tensor_copy(T.g2[:, gb:gb + w], T.stt[:, 0:64].indirect(off))))
+        need("v", "vec", i)
+        i_n = V(v.tensor_tensor_scan(T.s1[:, gb:gb + w], T.rst[:, 0:w], T.g1[:, gb:gb + w], 0.0, A.max, A.add))
+        need("v", *st)
+        i_d = V(v.tensor_tensor(T.dl[:, gb:gb + w], T.nen[:, 0:64].indirect(off), T.g2[:, gb + 1:gb + w + 1], A.add))
+        need("v", "vec", i_n)
+        i_e = V(v.tensor_copy(T.en0[:, eb:eb + R], T.s1[:, gb + 15:gb + w:16]))
+        need("v", "vec", max(i_d, i_e))
+        need("v", "act", max(i_vv[bt], i_fr))
+        i_s = V(v.tensor_copy(T.vv[:, vb:vb + WB * R].indirect(T.en0[:, eb:eb + R]), T.dl[:, gb:gb + w]))
+        return i_n, i_s, fill and fill()
+
+    def offsets(bt, bs, i_s, fill=None):
+        need("v", "vec", i_s)
+        i1 = []
+        for b in bs:
+            p, c = 128 * (PB[bt] + b), VB[bt] + WB * b
+            i1.append(V(v.tensor_tensor_scan(T.la[:, p:p + 128], T.fr[:], T.vv[:, c:c + 128],
+                                             T.g2[:, GB[bt] + 16 * b:GB[bt] + 16 * b + 1], A.add, A.add)))
+        for b, i in zip(bs, i1):
+            p = 128 * (PB[bt] + b)
+            need("v", "vec", i)
+            i2 = V(v.tensor_tensor_scan(T.lb[:, p:p + 128], T.dmk[:], T.la[:, p:p + 128], 0.0, A.add, A.max))
+        t, n = PB[bt] + bs[0], len(bs)
+        x = fill and fill()
+        need("v", "vec", i2)
+        return V(v.tensor_scalar(T.off[:, 32 * t:32 * (t + n)], T.lb[:, 128 * t + 3:128 * (t + n):4], T.cst[:], None, A.add)), x
+
+    def win(t):
+        return T.xs[:, :].indirect(T.off[:, 32 * t:32 * t + 32])
+
+    def gather_s(t, i):
+        need("s", "lx", 16)
+        need("s", "vec", i)
+        return S(sc.activation(T.tile[:, 512 * t:512 * t + 512], win(t), F.Copy))
+
+    def gather_v(t, i):
+        need("v", "lx", 16)
+        need("v", "vec", i)
+        return V(v.tensor_copy(T.tile[:, 512 * t:512 * t + 512], win(t)))
+
+    def quant(t, sem, i):
+        need("v", sem, i)
+        return V(v.quantize_mx(T.qc[:, 128 * t:128 * t + 128], T.qp[:, 128 * t:128 * t + 128],
+                               T.tile[:, 512 * t:512 * t + 512]))
+
+    def codes(t):
+        return u8(T.qc[:, 128 * t:128 * t + 128])
+
+    def plane(t):
+        return T.qp[:, 128 * t:128 * t + 128]
+
+    n_same = sum(len(lane_same(topo, T.cores[own[j]], core, at(own[j]))) for j in range(1, 4))
+    n_list = 4 * (len(topo.engines(hs[0], T.cores[oth[0]])) // 2)
+    n_ends = 4 * len(topo.engines(hs[0], T.cores[oth[0]]))
+
+    need("v", "cds", n_same)
+    need("s", "cds", n_same)
+    i_n, i_s, _ = ends("S", 3, T.cds[:, 0:3], True)
+    need("g", "vec", i_n)
+    fused([(T.cores[own[j]], T.el[:, at(own[j]) - 1:at(own[j])], T.s1[:, 16 * j - 1:16 * j], "ens",
+            lane_same(topo, core, T.cores[own[j]], j)) for j in range(1, 4)])
+    i0 = gather_s(0, offsets("S", [0], i_s)[0])
+    o, _ = offsets("S", [1, 2], i_s)
+    i1 = gather_s(1, o)
+    i2 = gather_s(2, o)
+    quant(0, "act", i0)
+
+    need("v", "cdo", n_list)
+    i_n, i_s, i_q = ends("O", 4, T.cdo[:, 0:4], False, lambda: quant(1, "act", i1))
+    need("g", "vec", i_n)
+    fused([(hs[k], T.hen[:, 0:1], T.s1[:, GB["O"] + 16 * k + 15:GB["O"] + 16 * k + 16], "hen", ends_up(topo, core, hs[k], k))
+           for k in range(4)])
+    i3 = gather_s(3, offsets("O", [0], i_s)[0])
+
+    def across(js, what, eng, put):
+        fused([(T.cores[own[j]], put(at(own[j]) - 1), what(j - 1), "t%d" % (at(own[j]) - 1),
+                eng(topo, core, T.cores[own[j]], j)) for j in js])
+
+    need("g", "vec", i_q)
+    across((1, 2), codes, codes_same, lambda s: u8(T.lc[:, 128 * s:128 * s + 128]))
+    o, i_q = offsets("O", [1, 2], i_s, lambda: quant(2, "act", i2))
+    i4 = gather_s(4, o)
+    i5 = gather_s(5, o)
+    need("g", "vec", i_q)
+    across((3,), codes, codes_same, lambda s: u8(T.lc[:, 128 * s:128 * s + 128]))
+    across((1, 2, 3), plane, plane_same, lambda s: T.lp[:, 128 * s:128 * s + 128])
+
+    def up(ks, via, put, sem):
+        fused([(hs[k], u8(T.hc[:, 0:128]), codes(3 + k), "hc", codes_up(topo, core, hs[k], k)) for k in ks])
+        fused([(hs[h], put, plane(3 + k), sem, plane_up(topo, core, hs[h], k)) for k, h in zip(ks, via)])
+
+    o, _ = offsets("O", [3], i_s, lambda: quant(3, "act", i3))
+    i = quant(4, "act", i4)
+    need("g", "vec", i)
+    up((0, 1), (0, 1), T.hp[:, 0:128], "hp")
+    i6 = gather_v(6, o)
+    quant(5, "act", i5)
+    i = quant(6, "vec", i6)
+    need("g", "vec", i)
+    up((3, 2), (0, 1), T.hp[:, 128:256], "hq")
+
+    need("v", "lw", 16)
+    i_w = V(v.quantize_mx(T.wc[:], T.wp[:], T.ws[:]))
+    i_l = V(v.tensor_copy(T.cdm[:, 0:1], T.cdu[:, rank:rank + 1]))
+    need("v", "vec", i_l)
+    need("s", "vec", i_l)
+    _, i_s, _ = ends("M", 1, T.cdm[:, 0:1], True)
+
+    order = [2, 1, 0, 7, 3, 6, 4, 5]
+    first = {2: 0, 1: 0, 0: 0, 7: 3, 3: 4, 6: 4, 4: 4, 5: 4}
+    col = [0, 1, 2, 4, 6, 7, 8, 9]
+
+    def places(slots, sem, val):
+        need("s", sem, val)
+        for s in slots:
+            p = order.index(s)
+            b = (-(s + 1)) % 4 - 1 if s < 3 else (3 - s) % 4
+            i = S(sc.activation(T.ef[:, col[p]:col[p] + 1], T.el[:, s:s + 1], F.Copy,
+                                bias=float(128 * (p - first[s]) - WB * b - 1)))
+        return i
+
+    def last(slots, i):
+        c = col[order.index(slots[0])]
+        need("v", "act", i)
+        return V(v.tensor_copy(T.en[:, c:c + len(slots)], T.ef[:, c:c + len(slots)]))
+
+    def border(slots):
+        p, n = order.index(slots[0]), len(slots)
+        return V(v.tensor_copy(T.mk[:, 128 * p + 8:128 * (p + n) + 8].indirect(T.en[:, col[p]:col[p] + n]), T.neg[:, 0:16 * n]))
+
+    i_f = places((2, 1, 0), "ens", n_same)
+    i7 = gather_s(7, offsets("M", [0], i_s)[0])
+    i_g = places((3, 6, 4, 5), "eno", n_ends)
+    V(v.tensor_scalar(T.en[:, 4:5], T.s1[:, GB["M"] + 15:GB["M"] + 16], -1.0, None, A.add))
+    i = last((2, 1, 0), i_f)
+    need("v", "act", i_mk)
+    need("v", "vec", i)
+    i_b = [border((2, 1, 0)), border((7,))]
+
+    def tile_engines(s):
+        if s >= 3:
+            return 2 * len(topo.engines(hs[0], T.cores[oth[0]]))
+        j = (-(s + 1)) % 4
+        return sum(len(f(topo, T.cores[own[s + 1]], core, j)) for f in (codes_same, plane_same))
+
+    def score(slots):
+        for s in slots:
+            p = order.index(s)
+            ps = T.ps[:, 512 * s:512 * s + 128]
+            need("t", "vec", i_w)
+            if s == 7:
+                need("t", "vec", i_own)
+                i = done("pe", pe.matmul_mx(ps, T.wc[:], T.wp[:], T.qc[:, 896:1024], T.qp[:, 896:1024], True, True))
+            else:
+                need("t", "t%d" % s, tile_engines(s))
+                i = done("pe", pe.matmul_mx(ps, T.wc[:], T.wp[:], T.lc[:, 128 * s:128 * s + 128],
+                                            T.lp[:, 128 * s:128 * s + 128], True, True))
+            need("v", "pe", i)
+            need("v", "vec", i_b[-1])
+            i = V(v.tensor_tensor_scan(T.so[:, 128 * p:128 * p + 128], T.mk[:, 128 * p + 7:128 * p + 135], ps, -BIG, A.min, A.max))
+        need("s", "vec", i)
+        p, n, f = order.index(slots[0]), len(slots), first[slots[0]]
+        i = S(sc.activation(T.ys[:, 16 * p:16 * (p + n)], T.so[:, 128 * f:128 * (p + n)].indirect(T.en[:, col[p]:col[p] + n]), F.Copy))
+        need("y", "act", i)
+        for s in slots:
+            p = order.index(s)
+            q = rank if s == 7 else own[s + 1] if s < 3 else oth[s - 3]
+            g.sync.dma_start(T.y[:, 16 * q:16 * q + 16], T.ys[:, 16 * p:16 * p + 16]).then_inc(T.sem.ly, 16)
+
+    score((2, 1, 0))
+    i_own = quant(7, "act", i7)
+    score((7,))
+    i = last((3, 6, 4, 5), i_g)
+    need("v", "vec", i)
+    i_b.append(border((3, 6, 4, 5)))
+    score((3, 6))
+    score((4, 5))
+
+    for sem in ("vec", "act", "pe", "gc", "sent"):
+        need("g", sem, cnt[sem])
+    need("g", "ly", 128)

@@ -1,52 +1,65 @@
 from concourse.bass import DstId, RemoteDMATransfer
 from concourse.mybir import dt, AluOpType as A, ActivationFunctionType as F
 
-N, TOK, CAP = 8, 512, 128
+N, ND, TOK, CAP = 8, 64, 512, 128
 BIG, FAR, LIFT = 1.0e29, 1.0e6, 4096.0
 WB = 136
-VB = {"S": 0, "O": 408, "M": 952}
-GB = {"S": 0, "O": 56, "M": 128}
+WX = 520
+VB = {"S": 0, "O": 408, "M": 680}
+GB = {"S": 0, "O": 56, "M": 96}
 EB = {"S": 0, "O": 4, "M": 8}
-PB = {"S": 0, "O": 3, "M": 7}
-CARRY = {0: (0, 3), 1: (1, 2)}
+PB = {"S": 0, "O": 3, "M": 5}
 
 SCRATCH = {
-    "cdi": ("sbuf", [128, 8], "int32"), "cdu": ("sbuf", [128, 8], "uint16"), "cdm": ("sbuf", [128, 2], "uint16"),
+    "cdi": ("sbuf", [128, 8], "int32"), "cdu": ("sbuf", [128, 8], "uint16"), "cdf": ("sbuf", [128, 8], "float32"),
+    "cdm": ("sbuf", [128, 2], "uint16"), "tci": ("sbuf", [128, 1], "int32"), "pk": ("sbuf", [128, 2], "uint16"),
     "row": ("sbuf", [1, 128], "int32"), "tab": ("sbuf", [128, 128], "int32"),
     "stt": ("sbuf", [128, 64], "float32"), "lnt": ("sbuf", [128, 64], "float32"),
     "nes": ("sbuf", [128, 64], "float32"), "nen": ("sbuf", [128, 64], "float32"),
     "poi": ("sbuf", [128, 4], "int32"), "poa": ("sbuf", [128, 4], "int32"), "pou": ("sbuf", [128, 4], "uint16"),
     "pp": ("sbuf", [128, 1], "int32"), "ki": ("sbuf", [128, 3], "int32"), "kf": ("sbuf", [128, 3], "float32"),
-    "csu": ("sbuf", [128, 1], "float32"), "cst": ("sbuf", [128, 1], "float32"), "zz": ("sbuf", [128, 1032], "bfloat16"),
-    "ii": ("sbuf", [128, 64], "float32"), "jj": ("sbuf", [128, 128], "float32"),
-    "le": ("sbuf", [128, 64], "float32"), "dmb": ("sbuf", [128, 128], "float32"), "dmk": ("sbuf", [128, 128], "float32"),
-    "rst": ("sbuf", [128, 64], "float32"), "fr": ("sbuf", [128, 128], "float32"), "neg": ("sbuf", [128, 64], "float32"),
-    "cds": ("sbuf", [128, 4], "uint16"), "cdo": ("sbuf", [128, 4], "uint16"),
-    "g1": ("sbuf", [128, 152], "float32"), "s1": ("sbuf", [128, 152], "float32"), "g2": ("sbuf", [128, 152], "float32"),
-    "dl": ("sbuf", [128, 152], "float32"), "en0": ("sbuf", [128, 16], "uint16"),
-    "vv": ("sbuf", [128, 1088], "float32"),
-    "la": ("sbuf", [128, 1024], "float32"), "lb": ("sbuf", [128, 1024], "float32"),
-    "off": ("sbuf", [128, 256], "uint16"),
+    "csu": ("sbuf", [128, 1], "float32"), "cst": ("sbuf", [128, 1], "float32"), "zz": ("sbuf", [128, 816], "bfloat16"),
+    "ii": ("sbuf", [128, 48], "float32"), "jj": ("sbuf", [128, 128], "float32"),
+    "le": ("sbuf", [128, 48], "float32"), "dmb": ("sbuf", [128, 128], "float32"), "dmk": ("sbuf", [128, 128], "float32"),
+    "rst": ("sbuf", [128, 48], "float32"), "fr": ("sbuf", [128, 128], "float32"), "neg": ("sbuf", [128, 64], "float32"),
+    "cds": ("sbuf", [128, 4], "uint16"), "cdo": ("sbuf", [128, 2], "uint16"),
+    "g1": ("sbuf", [128, 120], "float32"), "s1": ("sbuf", [128, 120], "float32"), "g2": ("sbuf", [128, 120], "float32"),
+    "dl": ("sbuf", [128, 120], "float32"), "en0": ("sbuf", [128, 16], "uint16"),
+    "vv": ("sbuf", [128, 816], "float32"),
+    "la": ("sbuf", [128, 768], "float32"), "lb": ("sbuf", [128, 768], "float32"),
+    "off": ("sbuf", [128, 192], "uint16"),
     "xs": ("sbuf", [128, 4 * (TOK + CAP)], "bfloat16"), "ws": ("sbuf", [128, 512], "bfloat16"),
-    "tile": ("sbuf", [128, 4096], "bfloat16"),
-    "qc": ("sbuf", [128, 1024], "float8_e4m3fn_x4"), "qp": ("sbuf", [128, 1024], "uint8"),
-    "wc": ("sbuf", [128, 128], "float8_e4m3fn_x4"), "wp": ("sbuf", [128, 128], "uint8"),
-    "lc": ("sbuf", [128, 896], "float8_e4m3fn_x4"), "lp": ("sbuf", [128, 896], "uint8"),
-    "el": ("sbuf", [128, 8], "float32"), "ef": ("sbuf", [128, 12], "float32"), "en": ("sbuf", [128, 12], "uint16"),
-    "mk": ("sbuf", [128, 1032], "float32"), "so": ("sbuf", [128, 1024], "float32"), "ys": ("sbuf", [128, 128], "float32"),
-    "ps": ("psum", [128, 4096], "float32"),
-    "hcd": ("sbuf", [128, 8], "uint16"), "hen": ("sbuf", [128, 1], "float32"),
-    "hc": ("sbuf", [128, 128], "float8_e4m3fn_x4"), "hp": ("sbuf", [128, 256], "uint8"),
+    "tile": ("sbuf", [128, 3072], "bfloat16"),
+    "qc": ("sbuf", [128, 768], "float8_e4m3fn_x4"), "qp": ("sbuf", [128, 768], "uint8"),
+    "xc": ("sbuf", [128, 512], "float8_e4m3fn_x4"), "xp": ("sbuf", [128, 512], "uint8"),
+    "wc": ("sbuf", [128, 256], "float8_e4m3fn_x4"), "wp": ("sbuf", [128, 256], "uint8"),
+    "lc": ("sbuf", [128, 640], "float8_e4m3fn_x4"), "lp": ("sbuf", [128, 640], "uint8"),
+    "el": ("sbuf", [128, 8], "uint16"), "yr": ("sbuf", [128, 32], "float32"),
+    "mk": ("sbuf", [128, 816], "float32"), "so": ("sbuf", [128, 2 * WX], "float32"), "ys": ("sbuf", [128, 96], "float32"),
+    "ps": ("psum", [128, 3072], "float32"),
+    "hcd": ("sbuf", [128, 1], "uint16"), "hen": ("sbuf", [128, 2], "uint16"),
+    "hc": ("sbuf", [128, 128], "float8_e4m3fn_x4"), "hp": ("sbuf", [128, 128], "uint8"),
+    "hl": ("sbuf", [128, 2], "uint16"), "hli": ("sbuf", [128, 2], "int32"), "hlj": ("sbuf", [128, 2], "int32"),
+    "hlu": ("sbuf", [128, 4], "uint16"), "htb": ("sbuf", [128, 8], "uint16"), "htf": ("sbuf", [128, 8], "float32"),
+    "hef": ("sbuf", [128, 4], "float32"), "heu": ("sbuf", [128, 4], "uint16"), "hd": ("sbuf", [128, 128], "float32"),
 }
-SEMAPHORES = (["vec", "act", "pe", "gc", "lcd", "ltab", "lx", "lw", "ly", "sent", "cds", "cdo", "ens", "eno",
-               "hcd", "hen", "hc", "hp", "hq"] + ["t%d" % s for s in range(7)])
+SEMAPHORES = (["vec", "act", "pe", "gc", "lcd", "ltab", "ltc", "lx", "lw", "ly", "sent", "cds", "cdo", "ens", "eno",
+               "hcd", "hen", "hc", "hp", "hw", "hv", "hx", "hl", "hq0", "hq1", "r0", "r1"] + ["t%d" % s for s in range(5)])
 
 
 def groups(T, topo, r):
-    own = [q for q in range(N) if q == r or topo.may_write(T.cores[r], T.cores[q])]
-    oth = [q for q in range(N) if q not in own]
-    a = own.index(r)
-    return [own[(a + j) % len(own)] for j in range(len(own))], [oth[(a + k) % len(oth)] for k in range(len(oth))], a
+    def halves(u):
+        own = [q for q in range(N) if q == u or topo.may_write(T.cores[u], T.cores[q])]
+        oth = [q for q in range(N) if q not in own]
+        a = own.index(u)
+        rot = [oth[(a + k) % len(oth)] for k in range(len(oth))]
+        return [own[(a + j) % len(own)] for j in range(len(own))], rot[0::2], rot[1::2]
+
+    def mated(i):
+        return sum(topo.mates(T.cores[u], T.cores[q]) for u in range(N) for q in halves(u)[i])
+
+    own, ev, od = halves(r)
+    return (own, ev, od) if mated(1) >= mated(2) else (own, od, ev)
 
 
 def helpers(T, topo, r):
@@ -67,98 +80,28 @@ def bits(e):
     return sum(1 << x for x in e)
 
 
-def upper(topo, c, h):
-    e = topo.engines(c, h)
-    return e[len(e) // 2:]
+def upper(topo, c, h, k):
+    return part(part(topo.engines(c, h), 1, 2), k, 2)
 
 
-def lists_up(topo, c, h, k):
-    return part(upper(topo, c, h), k, 2)
+def half(topo, c, h, k):
+    return part(topo.engines(c, h), k, 2)
 
 
-def ends_up(topo, c, h, k):
-    return part(upper(topo, c, h), k, 4)
+def lane(topo, c, d, t):
+    return part(topo.engines(c, d), t, 4)
 
 
-def codes_up(topo, c, h, k):
-    return part(upper(topo, c, h), k, 2) if k in CARRY else part(topo.engines(c, h), k - 2, 2)
-
-
-def plane_up(topo, c, h, k):
-    return part(topo.engines(c, h), k, 4) if k in CARRY else part(topo.engines(c, h), k - 2, 2)
-
-
-def lane_same(topo, c, d, j):
-    return part(topo.engines(c, d), j - 1, 4)
-
-
-def codes_same(topo, c, d, j):
-    e = topo.engines(c, d)
-    return part(e, j - 1, 2) if j < 3 else e
-
-
-def plane_same(topo, c, d, j):
-    e = topo.engines(c, d)
-    return part(e, j - 1, 4) if j < 3 else part(e, 1, 2)
+def plane_same(topo, c, d, t):
+    return half(topo, c, d, t) if t < 2 else topo.engines(c, d)
 
 
 def u8(ap):
     return ap.bitcast(dt.uint8)
 
 
-def hand_on(g, core, T, topo, r, k):
-    _, oth, a = groups(T, topo, r)
-    rc = T.cores[r]
-    sent = [0]
-
-    def slot(n):
-        return (a - groups(T, topo, oth[n])[2]) % 4
-
-    def to(n):
-        return T.cores[oth[n]]
-
-    def on(n, dst, src, sem, eng):
-        rid, pid = topo.addr(to(n), core)
-        g.remote_dma(dst, src, T.sem[sem], T.sem.sent, pid, rid, bits(eng))
-        sent[0] += len(eng)
-
-    if k in CARRY:
-        g.wait_ge(T.sem.hcd, len(lists_up(topo, rc, core, k)))
-        ts = []
-        for i, n in enumerate(CARRY[k]):
-            rid, pid = topo.addr(to(n), core)
-            e = part(topo.engines(core, to(n)), i, 2)
-            ts.append(RemoteDMATransfer(dst_ids=[DstId(rid=rid, pnc=pid)], dma_engine_mask=bits(e), remote_sem=T.sem.cdo,
-                                        src=T.hcd[:, oth[n]:oth[n] + 1], dst=T.cdo[:, slot(n):slot(n) + 1]))
-            sent[0] += len(e)
-        g.remote_dma_fused(ts, local_sem=T.sem.sent)
-    e = topo.engines(core, to(k))
-    g.wait_ge(T.sem.hen, len(ends_up(topo, rc, core, k)))
-    on(k, T.el[:, 3 + slot(k):4 + slot(k)], T.hen[:, 0:1], "eno", e)
-    s = 3 + slot(k)
-    g.wait_ge(T.sem.hc, len(codes_up(topo, rc, core, k)))
-    on(k, u8(T.lc[:, 128 * s:128 * s + 128]), u8(T.hc[:, 0:128]), "t%d" % s, e)
-    if k in CARRY:
-        for i, n in enumerate(CARRY[k]):
-            s = 3 + slot(n)
-            g.wait_ge(T.sem["hp" if i == 0 else "hq"], len(plane_up(topo, rc, core, n)))
-            on(n, T.lp[:, 128 * s:128 * s + 128], T.hp[:, 128 * i:128 * i + 128], "t%d" % s, topo.engines(core, to(n)))
-    g.wait_ge(T.sem.sent, sent[0])
-
-
-def rank_program(g, core, T, topo):
-    rank = T.rank_of(core)
-    if rank is None:
-        for r in range(N):
-            if T.cores[r] in topo.cores_of(core):
-                hs = helpers(T, topo, r)
-                if core in hs:
-                    hand_on(g, core, T, topo, r, hs.index(core))
-        return
-    own, oth, a = groups(T, topo, rank)
-    hs = helpers(T, topo, rank)
-    v, sc, pe = g.vector, g.scalar, g.tensor
-    queue = {"v": v, "s": sc, "t": pe, "g": g, "y": g.sync}
+def caller(g, core, T, topo):
+    queue = {"v": g.vector, "s": g.scalar, "t": g.tensor, "g": g, "y": g.sync}
     cnt = {"vec": 0, "act": 0, "pe": 0, "gc": 0, "sent": 0}
     seen = {}
 
@@ -172,42 +115,6 @@ def rank_program(g, core, T, topo):
         ins.then_inc(T.sem[sem], 1)
         return cnt[sem]
 
-    def V(ins):
-        return done("vec", ins)
-
-    def S(ins):
-        return done("act", ins)
-
-    for i in range(8):
-        (g.sync if i % 2 == 0 else sc).dma_start(T.cdi[16 * i:16 * i + 16, :], T.cd[:]).then_inc(T.sem.lcd, 16)
-    g.sync.dma_start(T.row[0:1, 0:64], T.st[:]).then_inc(T.sem.ltab, 16)
-    sc.dma_start(T.row[0:1, 64:128], T.ln[:]).then_inc(T.sem.ltab, 16)
-    g.sync.dma_start(T.xs[:, 0:4 * TOK], T.x[:]).then_inc(T.sem.lx, 16)
-    sc.dma_start(T.ws[:], T.qw[:]).then_inc(T.sem.lw, 16)
-
-    done("gc", g.iota(T.pp[:], [[0, 1]], 0, 1))
-    i_io = done("gc", g.iota(T.poi[:], [[1, 4]], 0, 4))
-    done("gc", g.iota(T.ii[:], [[0, 4], [1, 16]], 0, 0, allow_small_or_imprecise_dtypes=True))
-    done("gc", g.iota(T.jj[:], [[0, 32], [1, 4]], 0, 0, allow_small_or_imprecise_dtypes=True))
-
-    i_z = V(v.memset(T.zz[:], 0.0))
-    need("s", "vec", i_z)
-    i_vv = {}
-    for bt, R in (("S", 3), ("O", 4), ("M", 1)):
-        i_vv[bt] = S(sc.activation(T.vv[:, VB[bt]:VB[bt] + WB * R], T.zz[:, 0:WB * R], F.Copy))
-    i_fr = S(sc.activation(T.fr[:], T.zz[:, 0:128], F.Copy, bias=4.0))
-    S(sc.activation(T.neg[:], T.zz[:, 0:64], F.Copy, bias=-BIG))
-    i_mk = S(sc.activation(T.mk[:], T.zz[:], F.Copy, bias=BIG))
-    need("v", "gc", i_io)
-    V(v.tensor_scalar(T.ki[:, 0:1], T.pp[:], 15, None, A.bitwise_and))
-    V(v.tensor_scalar(T.ki[:, 1:2], T.pp[:], 3, None, A.bitwise_and))
-    V(v.tensor_scalar(T.ki[:, 2:3], T.pp[:], 15, 2, A.bitwise_and, A.arith_shift_right))
-    i_p = V(v.tensor_scalar(T.poa[:], T.poi[:], 63, None, A.bitwise_and))
-
-    need("v", "lcd", 128)
-    i_cd = V(v.tensor_copy(T.cdu[:], T.cdi[:]))
-    need("g", "vec", i_cd)
-
     def fused(trs):
         ts = []
         for dc, dst, src, sem, e in trs:
@@ -217,12 +124,165 @@ def rank_program(g, core, T, topo):
             cnt["sent"] += len(e)
         g.remote_dma_fused(ts, local_sem=T.sem.sent)
 
-    def at(d):
-        return (a - groups(T, topo, d)[2]) % 4
+    return need, done, fused, cnt
 
-    fused([(T.cores[own[j]], T.cds[:, at(own[j]) - 1:at(own[j])], T.cdu[:, own[j]:own[j] + 1], "cds",
-            lane_same(topo, core, T.cores[own[j]], j)) for j in range(1, 4)])
-    fused([(hs[k], T.hcd[:, 0:8], T.cdu[:, 0:8], "hcd", lists_up(topo, core, hs[k], k)) for k in CARRY])
+
+def score_all(g, T, need, done, n_tab, n_list, n_x, n_w):
+    v, sc, pe = g.vector, g.scalar, g.tensor
+
+    def V(ins):
+        return done("vec", ins)
+
+    V(v.memset(T.mk[:, 0:WX], BIG))
+    V(v.memset(T.neg[:], -BIG))
+    V(v.memset(T.so[:], 0.0))
+    for h, q in enumerate(("y", "s")):
+        need(q, "hcd", n_tab)
+        for i in range(8):
+            (g.sync, sc)[h].dma_start(T.htb[16 * i:16 * i + 16, 4 * h:4 * h + 4],
+                                      T.hcd[64 * h:64 * h + 64, 0:1]).then_inc(T.sem.ltab, 16)
+    need("v", "ltab", 256)
+    i = V(v.tensor_copy(T.htf[:], T.htb[:]))
+    need("v", "vec", i)
+    V(v.tensor_copy(T.mk[:, 0:WX].indirect(T.htb[:, 0:4]), T.neg[:]))
+    i = V(v.tensor_tensor(T.hef[:], T.htf[:, 0:4], T.htf[:, 4:8], A.add))
+    need("v", "vec", i)
+    V(v.tensor_copy(T.heu[:], T.hef[:]))
+    need("v", "hl", n_list)
+    i = V(v.tensor_copy(T.hli[:], T.hl[:]))
+    need("v", "vec", i)
+    V(v.tensor_scalar(T.hlj[:, 0:1], T.hli[:, 0:1], ND.bit_length() - 1, None, A.logical_shift_right))
+    i = V(v.tensor_scalar(T.hlj[:, 1:2], T.hli[:, 1:2], ND - 1, None, A.bitwise_and))
+    need("v", "vec", i)
+    i_l = V(v.tensor_copy(T.hlu[:, 0:4:2], T.hlj[:]))
+    need("t", "hx", n_x)
+    for n in range(2):
+        need("t", "hq%d" % n, n_w)
+        ps = T.ps[:, 512 * n:512 * n + TOK]
+        i = done("pe", pe.matmul_mx(ps, T.wc[:, 128 * n:128 * n + 128], T.wp[:, 128 * n:128 * n + 128], T.xc[:], T.xp[:],
+                                    True, True))
+        need("v", "vec", i_l)
+        need("v", "pe", i)
+        i = V(v.tensor_tensor_scan(T.so[:, WX * n + 1:WX * n + 1 + TOK], T.mk[:, 0:TOK], ps, -BIG, A.min, A.max))
+        need("s", "vec", i)
+        i = done("act", sc.activation(T.hd[:, 64 * n:64 * n + 64], T.so[:, WX * n:WX * n + WX].indirect(T.heu[:, 0:4]), F.Copy))
+        need("s", "act", i)
+        i = done("act", sc.activation(T.yr[:, 16 * n:16 * n + 16],
+                                      T.hd[:, 64 * n:64 * n + 64].indirect(T.hlu[:, 2 * n:2 * n + 1]), F.Copy))
+    return i
+
+
+def hand_on(g, core, T, topo, r, k):
+    _, til, sco = groups(T, topo, r)
+    rc = T.cores[r]
+    need, done, fused, cnt = caller(g, core, T, topo)
+    n = k % 2
+    to = T.cores[til[n]]
+    e = topo.engines(core, to)
+    n_up = len(upper(topo, rc, core, 0))
+    n_half = len(half(topo, rc, core, 0))
+
+    def back(m):
+        return groups(T, topo, sco[m])[2].index(r)
+
+    def scorer(m):
+        return helpers(T, topo, sco[m])[2]
+
+    if k < 2:
+        need("g", "hcd", n_up)
+        fused([(to, T.cdo[:, n:n + 1], T.hcd[:, 0:1], "cdo", e)])
+        b = back(k)
+        need("g", "hw", n_half)
+        fused([(scorer(k), u8(T.wc[:, 128 * b:128 * b + 128]), u8(T.wc[:, 0:128]), "hq%d" % b, e)])
+        need("g", "hv", n_half)
+        fused([(scorer(k), T.wp[:, 128 * b:128 * b + 128], T.wp[:, 0:128], "hq%d" % b, e)])
+        need("g", "hc", n_half)
+        fused([(to, u8(T.lc[:, 128 * (3 + n):128 * (4 + n)]), u8(T.hc[:]), "t%d" % (3 + n), e)])
+    else:
+        if k == 2:
+            i_y = score_all(g, T, need, done, n_up, len(e), 4 * n_half, 2 * len(e))
+            need("g", "hen", 2 * n_up)
+            fused([(T.cores[til[m]], T.el[:, EB["O"] + m:EB["O"] + m + 1], T.hen[:, m:m + 1], "eno", part(e, m, 2))
+                   for m in range(2)])
+        else:
+            need("g", "hcd", n_up)
+            fused([(scorer(m), T.hl[:, back(m):back(m) + 1], T.hcd[:, 0:1], "hl", part(e, m, 2)) for m in range(2)])
+        need("g", "hp", n_up)
+        fused([(to, T.lp[:, 128 * (3 + n):128 * (4 + n)], T.hp[:], "t%d" % (3 + n), e)])
+        if k == 2:
+            need("g", "act", i_y)
+            fused([(T.cores[sco[m]], T.yr[:, 16 * back(m):16 * back(m) + 16], T.yr[:, 16 * m:16 * m + 16], "r%d" % back(m),
+                    part(e, m, 2)) for m in range(2)])
+    for sem in cnt:
+        need("g", sem, cnt[sem])
+
+
+def rank_program(g, core, T, topo):
+    rank = T.rank_of(core)
+    if rank is None:
+        for r in range(N):
+            if T.cores[r] in topo.cores_of(core):
+                hs = helpers(T, topo, r)
+                if core in hs:
+                    hand_on(g, core, T, topo, r, hs.index(core))
+        return
+    own, til, sco = groups(T, topo, rank)
+    hs = helpers(T, topo, rank)
+    v, sc, pe = g.vector, g.scalar, g.tensor
+    need, done, fused, cnt = caller(g, core, T, topo)
+
+    def V(ins):
+        return done("vec", ins)
+
+    def S(ins):
+        return done("act", ins)
+
+    def dst(t):
+        return T.cores[own[t + 1]]
+
+    def src(t):
+        return own[3 - t]
+
+    for i in range(8):
+        (g.sync if i % 2 == 0 else sc).dma_start(T.cdi[16 * i:16 * i + 16, :], T.cd[:]).then_inc(T.sem.lcd, 16)
+    g.sync.dma_start(T.tci[0:64, :], T.st[:]).then_inc(T.sem.ltc, 16)
+    sc.dma_start(T.tci[64:128, :], T.ln[:]).then_inc(T.sem.ltc, 16)
+    g.sync.dma_start(T.row[0:1, 0:64], T.st[:]).then_inc(T.sem.ltab, 16)
+    sc.dma_start(T.row[0:1, 64:128], T.ln[:]).then_inc(T.sem.ltab, 16)
+    sc.dma_start(T.ws[:], T.qw[:]).then_inc(T.sem.lw, 16)
+    g.sync.dma_start(T.xs[:, 0:4 * TOK], T.x[:]).then_inc(T.sem.lx, 16)
+
+    done("gc", g.iota(T.pp[:], [[0, 1]], 0, 1))
+    i_io = done("gc", g.iota(T.poi[:], [[1, 4]], 0, 4))
+    done("gc", g.iota(T.ii[:], [[0, 3], [1, 16]], 0, 0, allow_small_or_imprecise_dtypes=True))
+    done("gc", g.iota(T.jj[:], [[0, 32], [1, 4]], 0, 0, allow_small_or_imprecise_dtypes=True))
+
+    i_z = V(v.memset(T.zz[:], 0.0))
+    need("s", "vec", i_z)
+    i_vv = S(sc.activation(T.vv[:], T.zz[:], F.Copy))
+    i_fr = S(sc.activation(T.fr[:], T.zz[:, 0:128], F.Copy, bias=4.0))
+    S(sc.activation(T.neg[:], T.zz[:, 0:64], F.Copy, bias=-BIG))
+    S(sc.activation(T.so[:, 0:816], T.zz[:], F.Copy))
+    i_mk = S(sc.activation(T.mk[:], T.zz[:], F.Copy, bias=BIG))
+    need("v", "gc", i_io)
+    V(v.tensor_scalar(T.ki[:, 0:1], T.pp[:], 15, None, A.bitwise_and))
+    V(v.tensor_scalar(T.ki[:, 1:2], T.pp[:], 3, None, A.bitwise_and))
+    V(v.tensor_scalar(T.ki[:, 2:3], T.pp[:], 15, 2, A.bitwise_and, A.arith_shift_right))
+    i_p = V(v.tensor_scalar(T.poa[:], T.poi[:], 63, None, A.bitwise_and))
+
+    need("v", "lcd", 128)
+    i_cd = V(v.tensor_copy(T.cdu[:], T.cdi[:]))
+    i = V(v.tensor_copy(T.cdf[:], T.cdi[:]))
+    need("v", "ltc", 32)
+    V(v.tensor_copy(T.pk[:, 1:2], T.tci[:]))
+    need("v", "vec", i)
+    i_pk = V(v.tensor_scalar(T.pk[:, 0:1], T.cdf[:, sco[1]:sco[1] + 1], float(ND), T.cdf[:, sco[0]:sco[0] + 1], A.mult, A.add))
+    need("g", "vec", i_cd)
+    fused([(hs[n], T.hcd[:, 0:1], T.cdu[:, til[n]:til[n] + 1], "hcd", upper(topo, core, hs[n], n)) for n in range(2)])
+    need("g", "vec", i_pk)
+    fused([(T.cores[src(t)], T.cds[:, t:t + 1], T.cdu[:, src(t):src(t) + 1], "cds", lane(topo, core, T.cores[src(t)], t))
+           for t in range(3)]
+          + [(hs[3 - n], T.hcd[:, 0:1], T.pk[:, n:n + 1], "hcd", upper(topo, core, hs[3 - n], n)) for n in range(2)])
     need("g", "ltab", 32)
     i_tab = done("gc", g.partition_broadcast(T.tab[:], T.row[0:1, :], 128))
 
@@ -236,7 +296,7 @@ def rank_program(g, core, T, topo):
     i_m = V(v.tensor_scalar(T.dmb[:], T.jj[:], T.kf[:, 2:3], FAR + LIFT, A.is_gt, A.mult))
     i_c = V(v.tensor_scalar(T.csu[:], T.kf[:, 2:3], -3.0, LIFT, A.add, A.mult))
     need("v", "vec", i_r)
-    for b in range(1, 4):
+    for b in range(1, 3):
         V(v.memset(T.rst[:, 16 * b:16 * b + 1], float(WB * b)))
     need("v", "vec", i_m)
     V(v.tensor_scalar(T.dmk[:], T.dmb[:], -FAR, None, A.add))
@@ -244,6 +304,8 @@ def rank_program(g, core, T, topo):
     V(v.tensor_scalar(T.cst[:], T.csu[:], T.kf[:, 1:2], -4.0, A.add, A.add))
     V(v.memset(T.g2[:], 0.0))
     V(v.memset(T.xs[:, 4 * TOK:], 0.0))
+    need("v", "lw", 16)
+    i_w = V(v.quantize_mx(T.wc[:, 0:128], T.wp[:, 0:128], T.ws[:]))
     need("v", "gc", i_tab)
     i_ln = V(v.tensor_copy(T.lnt[:], T.tab[:, 64:128].indirect(T.pou[:, 0:4])))
     i_st = V(v.tensor_scalar(T.stt[:], T.tab[:, 0:64].indirect(T.pou[:, 0:4]), 4.0, None, A.mult))
@@ -251,6 +313,15 @@ def rank_program(g, core, T, topo):
     i = V(v.tensor_scalar(T.nes[:], T.lnt[:], -4.0, None, A.mult))
     need("v", "vec", i)
     i_ne = V(v.tensor_tensor(T.nen[:], T.nes[:], T.stt[:], A.subtract))
+    need("v", "lx", 16)
+    i_x = V(v.quantize_mx(T.xc[:], T.xp[:], T.xs[:, 0:4 * TOK]))
+
+    need("g", "vec", i_w)
+    fused([(hs[n], u8(T.wc[:, 0:128]), u8(T.wc[:, 0:128]), "hw", half(topo, core, hs[n], n)) for n in range(2)])
+    fused([(hs[n], T.wp[:, 0:128], T.wp[:, 0:128], "hv", half(topo, core, hs[n], n)) for n in range(2)])
+    need("g", "vec", i_x)
+    fused([(hs[2], u8(T.xc[:]), u8(T.xc[:]), "hx", topo.engines(core, hs[2]))])
+    fused([(hs[2], T.xp[:], T.xp[:], "hx", topo.engines(core, hs[2]))])
 
     def ends(bt, R, off, on_s, fill=None):
         gb, eb, vb = GB[bt], EB[bt], VB[bt]
@@ -269,9 +340,9 @@ def rank_program(g, core, T, topo):
         need("v", "vec", i_n)
         i_e = V(v.tensor_copy(T.en0[:, eb:eb + R], T.s1[:, gb + 15:gb + w:16]))
         need("v", "vec", max(i_d, i_e))
-        need("v", "act", max(i_vv[bt], i_fr))
+        need("v", "act", max(i_vv, i_fr))
         i_s = V(v.tensor_copy(T.vv[:, vb:vb + WB * R].indirect(T.en0[:, eb:eb + R]), T.dl[:, gb:gb + w]))
-        return i_n, i_s, fill and fill()
+        return i_e, i_s, fill and fill()
 
     def offsets(bt, bs, i_s, fill=None):
         need("v", "vec", i_s)
@@ -298,7 +369,6 @@ def rank_program(g, core, T, topo):
         return S(sc.activation(T.tile[:, 512 * t:512 * t + 512], win(t), F.Copy))
 
     def gather_v(t, i):
-        need("v", "lx", 16)
         need("v", "vec", i)
         return V(v.tensor_copy(T.tile[:, 512 * t:512 * t + 512], win(t)))
 
@@ -313,133 +383,106 @@ def rank_program(g, core, T, topo):
     def plane(t):
         return T.qp[:, 128 * t:128 * t + 128]
 
-    n_same = sum(len(lane_same(topo, T.cores[own[j]], core, at(own[j]))) for j in range(1, 4))
-    n_list = 4 * (len(topo.engines(hs[0], T.cores[oth[0]])) // 2)
-    n_ends = 4 * len(topo.engines(hs[0], T.cores[oth[0]]))
+    def codes_across(t):
+        fused([(dst(t), u8(T.lc[:, 128 * t:128 * t + 128]), codes(t), "t%d" % t, topo.engines(core, dst(t)))])
+
+    def plane_across(t):
+        return dst(t), T.lp[:, 128 * t:128 * t + 128], plane(t), "t%d" % t, plane_same(topo, core, dst(t), t)
+
+    n_off = len(topo.engines(hs[0], T.cores[til[0]]))
+    n_same = sum(len(lane(topo, T.cores[src(t)], core, t)) for t in range(3))
 
     need("v", "cds", n_same)
     need("s", "cds", n_same)
-    i_n, i_s, _ = ends("S", 3, T.cds[:, 0:3], True)
-    need("g", "vec", i_n)
-    fused([(T.cores[own[j]], T.el[:, at(own[j]) - 1:at(own[j])], T.s1[:, 16 * j - 1:16 * j], "ens",
-            lane_same(topo, core, T.cores[own[j]], j)) for j in range(1, 4)])
-    i0 = gather_s(0, offsets("S", [0], i_s)[0])
-    o, _ = offsets("S", [1, 2], i_s)
-    i1 = gather_s(1, o)
+    _, s_s, _ = ends("S", 3, T.cds[:, 0:3], True)
+    i0 = gather_s(0, offsets("S", [0], s_s)[0])
+    i1 = gather_s(1, offsets("S", [1], s_s)[0])
+
+    need("v", "cdo", 2 * n_off)
+    i_e, s_o, i_q = ends("O", 2, T.cdo[:, 0:2], False, lambda: quant(0, "act", i0))
+    need("g", "vec", i_e)
+    fused([(dst(t), T.el[:, t:t + 1], T.en0[:, t:t + 1], "ens", lane(topo, core, dst(t), t)) for t in range(3)]
+          + [(hs[2], T.hen[:, n:n + 1], T.en0[:, EB["O"] + n:EB["O"] + n + 1], "hen", upper(topo, core, hs[2], n))
+             for n in range(2)])
+    need("g", "vec", i_q)
+    codes_across(0)
+    o, i_q = offsets("O", [0, 1], s_o, lambda: quant(1, "act", i1))
+    i3 = gather_s(3, o)
+    need("g", "vec", i_q)
+    codes_across(1)
+    i4 = gather_v(4, o)
+    o, _ = offsets("S", [2], s_s, lambda: quant(3, "act", i3))
     i2 = gather_s(2, o)
-    quant(0, "act", i0)
-
-    need("v", "cdo", n_list)
-    i_n, i_s, i_q = ends("O", 4, T.cdo[:, 0:4], False, lambda: quant(1, "act", i1))
-    need("g", "vec", i_n)
-    fused([(hs[k], T.hen[:, 0:1], T.s1[:, GB["O"] + 16 * k + 15:GB["O"] + 16 * k + 16], "hen", ends_up(topo, core, hs[k], k))
-           for k in range(4)])
-    i3 = gather_s(3, offsets("O", [0], i_s)[0])
-
-    def across(js, what, eng, put):
-        fused([(T.cores[own[j]], put(at(own[j]) - 1), what(j - 1), "t%d" % (at(own[j]) - 1),
-                eng(topo, core, T.cores[own[j]], j)) for j in js])
-
+    i_q = quant(4, "vec", i4)
     need("g", "vec", i_q)
-    across((1, 2), codes, codes_same, lambda s: u8(T.lc[:, 128 * s:128 * s + 128]))
-    o, i_q = offsets("O", [1, 2], i_s, lambda: quant(2, "act", i2))
-    i4 = gather_s(4, o)
-    i5 = gather_s(5, o)
-    need("g", "vec", i_q)
-    across((3,), codes, codes_same, lambda s: u8(T.lc[:, 128 * s:128 * s + 128]))
-    across((1, 2, 3), plane, plane_same, lambda s: T.lp[:, 128 * s:128 * s + 128])
+    fused([(hs[n], u8(T.hc[:]), codes(3 + n), "hc", half(topo, core, hs[n], n)) for n in range(2)])
+    fused([(hs[2 + n], T.hp[:], plane(3 + n), "hp", upper(topo, core, hs[2 + n], n)) for n in range(2)]
+          + [plane_across(t) for t in range(2)])
 
-    def up(ks, via, put, sem):
-        fused([(hs[k], u8(T.hc[:, 0:128]), codes(3 + k), "hc", codes_up(topo, core, hs[k], k)) for k in ks])
-        fused([(hs[h], put, plane(3 + k), sem, plane_up(topo, core, hs[h], k)) for k, h in zip(ks, via)])
-
-    o, _ = offsets("O", [3], i_s, lambda: quant(3, "act", i3))
-    i = quant(4, "act", i4)
-    need("g", "vec", i)
-    up((0, 1), (0, 1), T.hp[:, 0:128], "hp")
-    i6 = gather_v(6, o)
-    quant(5, "act", i5)
-    i = quant(6, "vec", i6)
-    need("g", "vec", i)
-    up((3, 2), (0, 1), T.hp[:, 128:256], "hq")
-
-    need("v", "lw", 16)
-    i_w = V(v.quantize_mx(T.wc[:], T.wp[:], T.ws[:]))
     i_l = V(v.tensor_copy(T.cdm[:, 0:1], T.cdu[:, rank:rank + 1]))
     need("v", "vec", i_l)
-    need("s", "vec", i_l)
-    _, i_s, _ = ends("M", 1, T.cdm[:, 0:1], True)
+    _, s_m, i_q = ends("M", 1, T.cdm[:, 0:1], False, lambda: quant(2, "act", i2))
+    need("g", "vec", i_q)
+    codes_across(2)
+    fused([plane_across(2)])
+    i5 = gather_s(5, offsets("M", [0], s_m)[0])
 
-    order = [2, 1, 0, 7, 3, 6, 4, 5]
-    first = {2: 0, 1: 0, 0: 0, 7: 3, 3: 4, 6: 4, 4: 4, 5: 4}
-    col = [0, 1, 2, 4, 6, 7, 8, 9]
+    batch = ["S", "S", "S", "O", "O", "M"]
 
-    def places(slots, sem, val):
-        need("s", sem, val)
-        for s in slots:
-            p = order.index(s)
-            b = (-(s + 1)) % 4 - 1 if s < 3 else (3 - s) % 4
-            i = S(sc.activation(T.ef[:, col[p]:col[p] + 1], T.el[:, s:s + 1], F.Copy,
-                                bias=float(128 * (p - first[s]) - WB * b - 1)))
-        return i
+    def last(s, n):
+        c = EB[batch[s]] + s - PB[batch[s]]
+        return (T.en0 if s == 5 else T.el)[:, c:c + n]
 
-    def last(slots, i):
-        c = col[order.index(slots[0])]
-        need("v", "act", i)
-        return V(v.tensor_copy(T.en[:, c:c + len(slots)], T.ef[:, c:c + len(slots)]))
+    def border(bt, R):
+        return V(v.tensor_copy(T.mk[:, VB[bt]:VB[bt] + WB * R].indirect(last(PB[bt], R)), T.neg[:, 0:16 * R]))
 
-    def border(slots):
-        p, n = order.index(slots[0]), len(slots)
-        return V(v.tensor_copy(T.mk[:, 128 * p + 8:128 * (p + n) + 8].indirect(T.en[:, col[p]:col[p] + n]), T.neg[:, 0:16 * n]))
-
-    i_f = places((2, 1, 0), "ens", n_same)
-    i7 = gather_s(7, offsets("M", [0], i_s)[0])
-    i_g = places((3, 6, 4, 5), "eno", n_ends)
-    V(v.tensor_scalar(T.en[:, 4:5], T.s1[:, GB["M"] + 15:GB["M"] + 16], -1.0, None, A.add))
-    i = last((2, 1, 0), i_f)
     need("v", "act", i_mk)
-    need("v", "vec", i)
-    i_b = [border((2, 1, 0)), border((7,))]
+    need("v", "ens", n_same)
+    border("S", 3)
+    border("M", 1)
+    need("v", "eno", n_off)
+    i_b = border("O", 2)
 
     def tile_engines(s):
         if s >= 3:
-            return 2 * len(topo.engines(hs[0], T.cores[oth[0]]))
-        j = (-(s + 1)) % 4
-        return sum(len(f(topo, T.cores[own[s + 1]], core, j)) for f in (codes_same, plane_same))
+            return 2 * n_off
+        return n_off + len(plane_same(topo, T.cores[src(s)], core, s))
+
+    def store(q, ap, on="y"):
+        (g.sync if on == "y" else sc).dma_start(T.y[:, 16 * q:16 * q + 16], ap).then_inc(T.sem.ly, 16)
 
     def score(slots):
+        bt = batch[slots[0]]
         for s in slots:
-            p = order.index(s)
+            c = VB[bt] + WB * (s - PB[bt])
             ps = T.ps[:, 512 * s:512 * s + 128]
             need("t", "vec", i_w)
-            if s == 7:
+            if s == 5:
                 need("t", "vec", i_own)
-                i = done("pe", pe.matmul_mx(ps, T.wc[:], T.wp[:], T.qc[:, 896:1024], T.qp[:, 896:1024], True, True))
+                i = done("pe", pe.matmul_mx(ps, T.wc[:, 0:128], T.wp[:, 0:128], T.qc[:, 640:768], T.qp[:, 640:768], True, True))
             else:
                 need("t", "t%d" % s, tile_engines(s))
-                i = done("pe", pe.matmul_mx(ps, T.wc[:], T.wp[:], T.lc[:, 128 * s:128 * s + 128],
+                i = done("pe", pe.matmul_mx(ps, T.wc[:, 0:128], T.wp[:, 0:128], T.lc[:, 128 * s:128 * s + 128],
                                             T.lp[:, 128 * s:128 * s + 128], True, True))
             need("v", "pe", i)
-            need("v", "vec", i_b[-1])
-            i = V(v.tensor_tensor_scan(T.so[:, 128 * p:128 * p + 128], T.mk[:, 128 * p + 7:128 * p + 135], ps, -BIG, A.min, A.max))
+            need("v", "vec", i_b)
+            i = V(v.tensor_tensor_scan(T.so[:, c + 1:c + 129], T.mk[:, c:c + 128], ps, -BIG, A.min, A.max))
         need("s", "vec", i)
-        p, n, f = order.index(slots[0]), len(slots), first[slots[0]]
-        i = S(sc.activation(T.ys[:, 16 * p:16 * (p + n)], T.so[:, 128 * f:128 * (p + n)].indirect(T.en[:, col[p]:col[p] + n]), F.Copy))
+        s, n = slots[0], len(slots)
+        i = S(sc.activation(T.ys[:, 16 * s:16 * (s + n)], T.so[:, VB[bt]:c + WB].indirect(last(s, n)), F.Copy))
         need("y", "act", i)
         for s in slots:
-            p = order.index(s)
-            q = rank if s == 7 else own[s + 1] if s < 3 else oth[s - 3]
-            g.sync.dma_start(T.y[:, 16 * q:16 * q + 16], T.ys[:, 16 * p:16 * p + 16]).then_inc(T.sem.ly, 16)
+            store(rank if s == 5 else src(s) if s < 3 else til[s - 3], T.ys[:, 16 * s:16 * s + 16])
 
-    score((2, 1, 0))
-    i_own = quant(7, "act", i7)
-    score((7,))
-    i = last((3, 6, 4, 5), i_g)
-    need("v", "vec", i)
-    i_b.append(border((3, 6, 4, 5)))
-    score((3, 6))
-    score((4, 5))
+    i_own = quant(5, "act", i5)
+    score((5,))
+    score((0, 1))
+    for m in range(2):
+        need("y", "r%d" % m, n_off // 2)
+        store(sco[m], T.yr[:, 16 * m:16 * m + 16])
+    score((3, 4))
+    score((2,))
 
-    for sem in ("vec", "act", "pe", "gc", "sent"):
+    for sem in cnt:
         need("g", sem, cnt[sem])
     need("g", "ly", 128)

@@ -1,50 +1,55 @@
 from concourse.bass import DstId, RemoteDMATransfer
-from concourse.mybir import dt, AluOpType as A, ActivationFunctionType as F
+from concourse.mybir import dt, AluOpType as A, ActivationFunctionType as F, AxisListType
 
-N, ND, TOK, CAP = 8, 64, 512, 128
+N, ND, TOK = 8, 64, 512
+HX = TOK // 2
 BIG, FAR, LIFT = 1.0e29, 1.0e6, 4096.0
+LOW = -3.0 * LIFT - 4.0
 WB = 136
 WX = 520
 VB = {"S": 0, "O": 408, "M": 680}
 GB = {"S": 0, "O": 56, "M": 96}
 EB = {"S": 0, "O": 4, "M": 8}
 PB = {"S": 0, "O": 3, "M": 5}
+CODES, PLANES = (0, 1), (2, 3)
 
 SCRATCH = {
     "cdi": ("sbuf", [128, 8], "int32"), "cdu": ("sbuf", [128, 8], "uint16"), "cdf": ("sbuf", [128, 8], "float32"),
     "cdm": ("sbuf", [128, 2], "uint16"), "tci": ("sbuf", [128, 1], "int32"), "pk": ("sbuf", [128, 2], "uint16"),
-    "row": ("sbuf", [1, 128], "int32"), "tab": ("sbuf", [128, 128], "int32"),
+    "row": ("sbuf", [1, 128], "int32"), "rowf": ("sbuf", [1, 128], "float32"), "tab": ("sbuf", [128, 128], "float32"),
     "stt": ("sbuf", [128, 64], "float32"), "lnt": ("sbuf", [128, 64], "float32"),
-    "nes": ("sbuf", [128, 64], "float32"), "nen": ("sbuf", [128, 64], "float32"),
+    "ent": ("sbuf", [128, 64], "float32"),
     "poi": ("sbuf", [128, 4], "int32"), "poa": ("sbuf", [128, 4], "int32"), "pou": ("sbuf", [128, 4], "uint16"),
-    "pp": ("sbuf", [128, 1], "int32"), "ki": ("sbuf", [128, 3], "int32"), "kf": ("sbuf", [128, 3], "float32"),
-    "csu": ("sbuf", [128, 1], "float32"), "cst": ("sbuf", [128, 1], "float32"), "zz": ("sbuf", [128, 816], "bfloat16"),
+    "ki": ("sbuf", [128, 2], "int32"), "kf": ("sbuf", [128, 2], "float32"),
+    "cst": ("sbuf", [128, 1], "float32"), "zz": ("sbuf", [128, 688], "bfloat16"),
     "ii": ("sbuf", [128, 48], "float32"), "jj": ("sbuf", [128, 128], "float32"),
     "le": ("sbuf", [128, 48], "float32"), "dmb": ("sbuf", [128, 128], "float32"), "dmk": ("sbuf", [128, 128], "float32"),
     "rst": ("sbuf", [128, 48], "float32"), "fr": ("sbuf", [128, 128], "float32"), "neg": ("sbuf", [128, 64], "float32"),
     "cds": ("sbuf", [128, 4], "uint16"), "cdo": ("sbuf", [128, 2], "uint16"),
     "g1": ("sbuf", [128, 120], "float32"), "s1": ("sbuf", [128, 120], "float32"), "g2": ("sbuf", [128, 120], "float32"),
     "dl": ("sbuf", [128, 120], "float32"), "en0": ("sbuf", [128, 16], "uint16"),
-    "vv": ("sbuf", [128, 816], "float32"),
-    "la": ("sbuf", [128, 768], "float32"), "lb": ("sbuf", [128, 768], "float32"),
-    "off": ("sbuf", [128, 192], "uint16"),
-    "xs": ("sbuf", [128, 4 * (TOK + CAP)], "bfloat16"), "ws": ("sbuf", [128, 512], "bfloat16"),
+    "vv": ("sbuf", [128, 680], "float32"),
+    "la": ("sbuf", [128, 640], "float32"), "lb": ("sbuf", [128, 640], "float32"),
+    "off": ("sbuf", [128, 160], "uint16"),
+    "xs": ("sbuf", [128, 4 * TOK], "bfloat16"), "ws": ("sbuf", [128, 512], "bfloat16"),
     "tile": ("sbuf", [128, 3072], "bfloat16"),
     "qc": ("sbuf", [128, 768], "float8_e4m3fn_x4"), "qp": ("sbuf", [128, 768], "uint8"),
     "xc": ("sbuf", [128, 512], "float8_e4m3fn_x4"), "xp": ("sbuf", [128, 512], "uint8"),
     "wc": ("sbuf", [128, 256], "float8_e4m3fn_x4"), "wp": ("sbuf", [128, 256], "uint8"),
     "lc": ("sbuf", [128, 640], "float8_e4m3fn_x4"), "lp": ("sbuf", [128, 640], "uint8"),
     "el": ("sbuf", [128, 8], "uint16"), "yr": ("sbuf", [128, 32], "float32"),
-    "mk": ("sbuf", [128, 816], "float32"), "so": ("sbuf", [128, 2 * WX], "float32"), "ys": ("sbuf", [128, 96], "float32"),
+    "eq": ("sbuf", [128, 16], "float32"), "og": ("sbuf", [128, 64], "float32"), "of": ("sbuf", [128, 4], "float32"),
+    "ou": ("sbuf", [128, 8], "uint16"), "mko": ("sbuf", [128, WX], "float32"),
+    "mk": ("sbuf", [128, 680], "float32"), "so": ("sbuf", [128, 680 + WX], "float32"), "ys": ("sbuf", [128, 96], "float32"),
     "ps": ("psum", [128, 3072], "float32"),
-    "hcd": ("sbuf", [128, 1], "uint16"), "hen": ("sbuf", [128, 2], "uint16"),
+    "hcd": ("sbuf", [128, 1], "uint16"), "hen": ("sbuf", [128, 1], "uint16"),
     "hc": ("sbuf", [128, 128], "float8_e4m3fn_x4"), "hp": ("sbuf", [128, 128], "uint8"),
-    "hl": ("sbuf", [128, 2], "uint16"), "hli": ("sbuf", [128, 2], "int32"), "hlj": ("sbuf", [128, 2], "int32"),
-    "hlu": ("sbuf", [128, 4], "uint16"), "htb": ("sbuf", [128, 8], "uint16"), "htf": ("sbuf", [128, 8], "float32"),
-    "hef": ("sbuf", [128, 4], "float32"), "heu": ("sbuf", [128, 4], "uint16"), "hd": ("sbuf", [128, 128], "float32"),
+    "htd": ("dram", [128, 1], "uint16"),
+    "hl": ("sbuf", [128, 2], "uint16"), "hli": ("sbuf", [128, 2], "int32"), "hlj": ("sbuf", [128, 4], "int32"),
+    "hlf": ("sbuf", [128, 4], "float32"), "hlu": ("sbuf", [128, 4], "uint16"), "hrow": ("sbuf", [1, 128], "uint16"),
 }
-SEMAPHORES = (["vec", "act", "pe", "gc", "lcd", "ltab", "ltc", "lx", "lw", "ly", "sent", "cds", "cdo", "ens", "eno",
-               "hcd", "hen", "hc", "hp", "hw", "hv", "hx", "hl", "hq0", "hq1", "r0", "r1"] + ["t%d" % s for s in range(5)])
+SEMAPHORES = (["vec", "act", "pe", "gc", "lcd", "ltab", "ltc", "lx0", "lx1", "lw", "ly", "sent", "cds", "cdo", "ens", "eno",
+               "hcd", "htb", "hen", "hc", "hp", "hw", "hv", "hx0", "hx1", "hl", "hq0", "hq1", "r0", "r1"] + ["t%d" % s for s in range(5)])
 
 
 def groups(T, topo, r):
@@ -80,8 +85,8 @@ def bits(e):
     return sum(1 << x for x in e)
 
 
-def upper(topo, c, h, k):
-    return part(part(topo.engines(c, h), 1, 2), k, 2)
+def upper(topo, c, h, k, n=2):
+    return part(part(topo.engines(c, h), 1, 2), k, n)
 
 
 def half(topo, c, h, k):
@@ -93,7 +98,7 @@ def lane(topo, c, d, t):
 
 
 def plane_same(topo, c, d, t):
-    return half(topo, c, d, t) if t < 2 else topo.engines(c, d)
+    return topo.engines(c, d)
 
 
 def u8(ap):
@@ -127,53 +132,75 @@ def caller(g, core, T, topo):
     return need, done, fused, cnt
 
 
-def score_all(g, T, need, done, n_tab, n_list, n_x, n_w):
+def score_all(g, T, need, done, i_io, n_tab, n_list, n_x, n_w):
     v, sc, pe = g.vector, g.scalar, g.tensor
 
     def V(ins):
         return done("vec", ins)
 
-    V(v.memset(T.mk[:, 0:WX], BIG))
+    mk = (T.mk, T.mko)
+    for n in range(2):
+        V(v.memset(mk[n][:, 0:WX], BIG))
     V(v.memset(T.neg[:], -BIG))
-    V(v.memset(T.so[:], 0.0))
-    for h, q in enumerate(("y", "s")):
-        need(q, "hcd", n_tab)
-        for i in range(8):
-            (g.sync, sc)[h].dma_start(T.htb[16 * i:16 * i + 16, 4 * h:4 * h + 4],
-                                      T.hcd[64 * h:64 * h + 64, 0:1]).then_inc(T.sem.ltab, 16)
-    need("v", "ltab", 256)
-    i = V(v.tensor_copy(T.htf[:], T.htb[:]))
+    V(v.memset(T.so[:, 0:2 * WX], 0.0))
+    need("v", "gc", i_io)
+    i = V(v.tensor_scalar(T.ki[:, 0:1], T.poi[:, 0:1], 15, None, A.bitwise_and))
     need("v", "vec", i)
-    V(v.tensor_copy(T.mk[:, 0:WX].indirect(T.htb[:, 0:4]), T.neg[:]))
-    i = V(v.tensor_tensor(T.hef[:], T.htf[:, 0:4], T.htf[:, 4:8], A.add))
+    i = V(v.tensor_copy(T.kf[:, 0:1], T.ki[:, 0:1]))
     need("v", "vec", i)
-    V(v.tensor_copy(T.heu[:], T.hef[:]))
+    V(v.tensor_scalar(T.eq[:], T.ii[:, 0:16], T.kf[:, 0:1], None, A.is_equal))
+    need("y", "htb", n_tab)
+    g.sync.dma_start(T.hrow[0:1, :], T.htd[:]).then_inc(T.sem.ltab, 16)
+    need("v", "ltab", 16)
+    i = V(v.tensor_copy(T.rowf[0:1, :], T.hrow[0:1, :]))
+    need("v", "vec", i)
+    need("g", "vec", V(v.tensor_tensor(T.rowf[0:1, 64:128], T.rowf[0:1, 64:128], T.rowf[0:1, 0:64], A.add)))
+    i_tab = done("gc", g.partition_broadcast(T.tab[:], T.rowf[0:1, :], 128))
     need("v", "hl", n_list)
     i = V(v.tensor_copy(T.hli[:], T.hl[:]))
     need("v", "vec", i)
-    V(v.tensor_scalar(T.hlj[:, 0:1], T.hli[:, 0:1], ND.bit_length() - 1, None, A.logical_shift_right))
-    i = V(v.tensor_scalar(T.hlj[:, 1:2], T.hli[:, 1:2], ND - 1, None, A.bitwise_and))
+    for n, low in enumerate((6, 0)):
+        V(v.tensor_scalar(T.hlj[:, n:n + 1], T.hli[:, n:n + 1], low, 15, A.logical_shift_right, A.bitwise_and))
+        i = V(v.tensor_scalar(T.hlj[:, 2 + n:3 + n], T.hli[:, n:n + 1], low + 4, 3, A.logical_shift_right, A.bitwise_and))
     need("v", "vec", i)
-    i_l = V(v.tensor_copy(T.hlu[:, 0:4:2], T.hlj[:]))
-    need("t", "hx", n_x)
+    i = V(v.tensor_copy(T.hlf[:], T.hlj[:]))
+    need("v", "vec", i)
     for n in range(2):
+        i = V(v.tensor_scalar(T.hlu[:, 2 * n:2 * n + 1], T.hlf[:, n:n + 1], 4.0, T.hlf[:, 2 + n:3 + n], A.mult, A.add))
+    need("v", "vec", i)
+    need("v", "gc", i_tab)
+    for j in range(4):
+        i = V(v.tensor_tensor(T.og[:, 16 * j:16 * j + 16], T.tab[:, 64 * (j % 2):64 * (j % 2) + 64].indirect(
+            T.hlu[:, 2 * (j // 2):2 * (j // 2) + 1]), T.eq[:], A.mult))
+    need("v", "vec", i)
+    for j in range(4):
+        i = V(v.tensor_reduce(T.of[:, j:j + 1], T.og[:, 16 * j:16 * j + 16], AxisListType.X, A.add))
+    need("v", "vec", i)
+    i = V(v.tensor_copy(T.ou[:, 0:8:2], T.of[:]))
+    need("v", "vec", i)
+    for n in range(2):
+        i_l = V(v.tensor_copy(mk[n][:, 0:WX].indirect(T.ou[:, 4 * n:4 * n + 1]), T.neg[:, 0:16]))
+    i_s = [i_l, i_l]
+    for h, n in ((0, 0), (0, 1), (1, 0), (1, 1)):
+        need("t", "hx%d" % h, n_x // (1 + h))
         need("t", "hq%d" % n, n_w)
-        ps = T.ps[:, 512 * n:512 * n + TOK]
-        i = done("pe", pe.matmul_mx(ps, T.wc[:, 128 * n:128 * n + 128], T.wp[:, 128 * n:128 * n + 128], T.xc[:], T.xp[:],
-                                    True, True))
-        need("v", "vec", i_l)
+        ps = T.ps[:, 512 * (2 * h + n):512 * (2 * h + n) + HX]
+        i = done("pe", pe.matmul_mx(ps, T.wc[:, 128 * n:128 * n + 128], T.wp[:, 128 * n:128 * n + 128],
+                                    T.xc[:, HX * h:HX * h + HX], T.xp[:, HX * h:HX * h + HX], True, True))
+        need("v", "vec", i_s[n])
         need("v", "pe", i)
-        i = V(v.tensor_tensor_scan(T.so[:, WX * n + 1:WX * n + 1 + TOK], T.mk[:, 0:TOK], ps, -BIG, A.min, A.max))
-        need("s", "vec", i)
-        i = done("act", sc.activation(T.hd[:, 64 * n:64 * n + 64], T.so[:, WX * n:WX * n + WX].indirect(T.heu[:, 0:4]), F.Copy))
-        need("s", "act", i)
+        c = WX * n + HX * h
+        i_s[n] = V(v.tensor_tensor_scan(T.so[:, c + 1:c + 1 + HX], mk[n][:, HX * h:HX * h + HX], ps,
+                                        T.so[:, c:c + 1] if h else -BIG, A.min, A.max))
+    for n in range(2):
+        need("s", "vec", i_s[n])
         i = done("act", sc.activation(T.yr[:, 16 * n:16 * n + 16],
-                                      T.hd[:, 64 * n:64 * n + 64].indirect(T.hlu[:, 2 * n:2 * n + 1]), F.Copy))
+                                      T.so[:, WX * n:WX * n + WX].indirect(T.ou[:, 4 * n + 2:4 * n + 3]), F.Copy))
     return i
 
 
 def hand_on(g, core, T, topo, r, k):
-    _, til, sco = groups(T, topo, r)
+    own, til, sco = groups(T, topo, r)
     rc = T.cores[r]
     need, done, fused, cnt = caller(g, core, T, topo)
     n = k % 2
@@ -194,25 +221,32 @@ def hand_on(g, core, T, topo, r, k):
         b = back(k)
         need("g", "hw", n_half)
         fused([(scorer(k), u8(T.wc[:, 128 * b:128 * b + 128]), u8(T.wc[:, 0:128]), "hq%d" % b, e)])
-        need("g", "hv", n_half)
-        fused([(scorer(k), T.wp[:, 128 * b:128 * b + 128], T.wp[:, 0:128], "hq%d" % b, e)])
-        need("g", "hc", n_half)
-        fused([(to, u8(T.lc[:, 128 * (3 + n):128 * (4 + n)]), u8(T.hc[:]), "t%d" % (3 + n), e)])
+        need("g", "hen", n_up)
+        fused([(to, T.el[:, EB["O"] + n:EB["O"] + n + 1], T.hen[:], "eno", e)])
+    elif k == 2:
+        done("gc", g.iota(T.poi[:, 0:1], [[0, 1]], 0, 1))
+        i_io = done("gc", g.iota(T.ii[:, 0:16], [[1, 16]], 0, 0, allow_small_or_imprecise_dtypes=True))
+        need("g", "hcd", n_up)
+        fused([(scorer(m), T.hl[:, back(m):back(m) + 1], T.hcd[:, 0:1], "hl", part(e, m, 2)) for m in range(2)])
+        i_y = score_all(g, T, need, done, i_io, n_up, len(e), 4 * n_half, len(e) + len(e) // 2)
     else:
-        if k == 2:
-            i_y = score_all(g, T, need, done, n_up, len(e), 4 * n_half, 2 * len(e))
-            need("g", "hen", 2 * n_up)
-            fused([(T.cores[til[m]], T.el[:, EB["O"] + m:EB["O"] + m + 1], T.hen[:, m:m + 1], "eno", part(e, m, 2))
-                   for m in range(2)])
-        else:
-            need("g", "hcd", n_up)
-            fused([(scorer(m), T.hl[:, back(m):back(m) + 1], T.hcd[:, 0:1], "hl", part(e, m, 2)) for m in range(2)])
+        need("g", "hv", 2 * n_half)
+        fused([(scorer(m), T.wp[:, 128 * back(m):128 * back(m) + 128], T.wp[:, 0:128], "hq%d" % back(m), part(e, m, 2))
+               for m in range(2)])
+        need("g", "hc", n_half)
+        fused([(T.cores[own[1]], u8(T.lc[:, 0:128]), u8(T.hc[:]), "t0", e)])
+    if k in CODES:
+        n = CODES.index(k)
+        need("g", "hc", n_half)
+        fused([(T.cores[til[n]], u8(T.lc[:, 128 * (3 + n):128 * (4 + n)]), u8(T.hc[:]), "t%d" % (3 + n), e)])
+    if k in PLANES:
+        n = PLANES.index(k)
         need("g", "hp", n_up)
-        fused([(to, T.lp[:, 128 * (3 + n):128 * (4 + n)], T.hp[:], "t%d" % (3 + n), e)])
-        if k == 2:
-            need("g", "act", i_y)
-            fused([(T.cores[sco[m]], T.yr[:, 16 * back(m):16 * back(m) + 16], T.yr[:, 16 * m:16 * m + 16], "r%d" % back(m),
-                    part(e, m, 2)) for m in range(2)])
+        fused([(T.cores[til[n]], T.lp[:, 128 * (3 + n):128 * (4 + n)], T.hp[:], "t%d" % (3 + n), e)])
+    if k == 2:
+        need("g", "act", i_y)
+        fused([(T.cores[sco[m]], T.yr[:, 16 * back(m):16 * back(m) + 16], T.yr[:, 16 * m:16 * m + 16], "r%d" % back(m),
+                part(e, m, 2)) for m in range(2)])
     for sem in cnt:
         need("g", sem, cnt[sem])
 
@@ -245,90 +279,89 @@ def rank_program(g, core, T, topo):
 
     for i in range(8):
         (g.sync if i % 2 == 0 else sc).dma_start(T.cdi[16 * i:16 * i + 16, :], T.cd[:]).then_inc(T.sem.lcd, 16)
-    g.sync.dma_start(T.tci[0:64, :], T.st[:]).then_inc(T.sem.ltc, 16)
-    sc.dma_start(T.tci[64:128, :], T.ln[:]).then_inc(T.sem.ltc, 16)
     g.sync.dma_start(T.row[0:1, 0:64], T.st[:]).then_inc(T.sem.ltab, 16)
     sc.dma_start(T.row[0:1, 64:128], T.ln[:]).then_inc(T.sem.ltab, 16)
+    g.sync.dma_start(T.tci[0:64, :], T.st[:]).then_inc(T.sem.ltc, 16)
+    sc.dma_start(T.tci[64:128, :], T.ln[:]).then_inc(T.sem.ltc, 16)
     sc.dma_start(T.ws[:], T.qw[:]).then_inc(T.sem.lw, 16)
-    g.sync.dma_start(T.xs[:, 0:4 * TOK], T.x[:]).then_inc(T.sem.lx, 16)
+    for h in range(2):
+        g.sync.dma_start(T.xs[:, 4 * HX * h:4 * HX * (h + 1)], T.x[:, 4 * HX * h:4 * HX * (h + 1)]).then_inc(T.sem["lx%d" % h], 16)
 
-    done("gc", g.iota(T.pp[:], [[0, 1]], 0, 1))
     i_io = done("gc", g.iota(T.poi[:], [[1, 4]], 0, 4))
     done("gc", g.iota(T.ii[:], [[0, 3], [1, 16]], 0, 0, allow_small_or_imprecise_dtypes=True))
     done("gc", g.iota(T.jj[:], [[0, 32], [1, 4]], 0, 0, allow_small_or_imprecise_dtypes=True))
+    i_ij = done("gc", g.iota(T.rst[:], [[WB, 3], [0, 16]], 0, 0, allow_small_or_imprecise_dtypes=True))
 
     i_z = V(v.memset(T.zz[:], 0.0))
     need("s", "vec", i_z)
-    i_vv = S(sc.activation(T.vv[:], T.zz[:], F.Copy))
+    i_vv = S(sc.activation(T.vv[:], T.zz[:, 0:680], F.Copy))
     i_fr = S(sc.activation(T.fr[:], T.zz[:, 0:128], F.Copy, bias=4.0))
-    S(sc.activation(T.neg[:], T.zz[:, 0:64], F.Copy, bias=-BIG))
-    S(sc.activation(T.so[:, 0:816], T.zz[:], F.Copy))
-    i_mk = S(sc.activation(T.mk[:], T.zz[:], F.Copy, bias=BIG))
+    V(v.memset(T.g2[:], LOW))
     need("v", "gc", i_io)
-    V(v.tensor_scalar(T.ki[:, 0:1], T.pp[:], 15, None, A.bitwise_and))
-    V(v.tensor_scalar(T.ki[:, 1:2], T.pp[:], 3, None, A.bitwise_and))
-    V(v.tensor_scalar(T.ki[:, 2:3], T.pp[:], 15, 2, A.bitwise_and, A.arith_shift_right))
+    V(v.tensor_scalar(T.ki[:, 0:1], T.poi[:, 0:1], 63, 2, A.bitwise_and, A.arith_shift_right))
+    V(v.tensor_scalar(T.ki[:, 1:2], T.poi[:, 0:1], 63, 4, A.bitwise_and, A.arith_shift_right))
     i_p = V(v.tensor_scalar(T.poa[:], T.poi[:], 63, None, A.bitwise_and))
+    need("v", "vec", i_p)
+    V(v.tensor_copy(T.kf[:], T.ki[:]))
+    i_k = V(v.tensor_copy(T.pou[:], T.poa[:]))
 
     need("v", "lcd", 128)
     i_cd = V(v.tensor_copy(T.cdu[:], T.cdi[:]))
     i = V(v.tensor_copy(T.cdf[:], T.cdi[:]))
+    need("v", "ltab", 32)
+    i_row = V(v.tensor_copy(T.rowf[0:1, :], T.row[0:1, :]))
     need("v", "ltc", 32)
     V(v.tensor_copy(T.pk[:, 1:2], T.tci[:]))
     need("v", "vec", i)
     i_pk = V(v.tensor_scalar(T.pk[:, 0:1], T.cdf[:, sco[1]:sco[1] + 1], float(ND), T.cdf[:, sco[0]:sco[0] + 1], A.mult, A.add))
     need("g", "vec", i_cd)
-    fused([(hs[n], T.hcd[:, 0:1], T.cdu[:, til[n]:til[n] + 1], "hcd", upper(topo, core, hs[n], n)) for n in range(2)])
-    need("g", "vec", i_pk)
     fused([(T.cores[src(t)], T.cds[:, t:t + 1], T.cdu[:, src(t):src(t) + 1], "cds", lane(topo, core, T.cores[src(t)], t))
            for t in range(3)]
-          + [(hs[3 - n], T.hcd[:, 0:1], T.pk[:, n:n + 1], "hcd", upper(topo, core, hs[3 - n], n)) for n in range(2)])
-    need("g", "ltab", 32)
-    i_tab = done("gc", g.partition_broadcast(T.tab[:], T.row[0:1, :], 128))
+          + [(hs[n], T.hcd[:, 0:1], T.cdu[:, til[n]:til[n] + 1], "hcd", upper(topo, core, hs[n], n)) for n in range(2)])
+    need("g", "vec", i_row)
+    i_tab = done("gc", g.partition_broadcast(T.tab[:], T.rowf[0:1, :], 128))
+    need("g", "vec", i_pk)
+    fused([(hs[2], (T.hcd, T.htd)[n][:], T.pk[:, n:n + 1], ("hcd", "htb")[n], upper(topo, core, hs[2], n)) for n in range(2)])
 
-    need("v", "vec", i_p)
-    V(v.tensor_copy(T.kf[:], T.ki[:]))
-    i_k = V(v.tensor_copy(T.pou[:], T.poa[:]))
-    i_r = V(v.memset(T.rst[:], 0.0))
-    need("v", "gc", 4)
+    need("v", "gc", i_ij)
     need("v", "vec", i_k)
-    V(v.tensor_scalar(T.le[:], T.ii[:], T.kf[:, 0:1], None, A.is_le))
-    i_m = V(v.tensor_scalar(T.dmb[:], T.jj[:], T.kf[:, 2:3], FAR + LIFT, A.is_gt, A.mult))
-    i_c = V(v.tensor_scalar(T.csu[:], T.kf[:, 2:3], -3.0, LIFT, A.add, A.mult))
-    need("v", "vec", i_r)
-    for b in range(1, 3):
-        V(v.memset(T.rst[:, 16 * b:16 * b + 1], float(WB * b)))
+    i_m = V(v.tensor_scalar(T.dmb[:], T.jj[:], T.kf[:, 1:2], FAR + LIFT, A.is_gt, A.mult))
+    V(v.tensor_scalar(T.le[:], T.ii[:], T.kf[:, 0:1], 0.25, A.is_le, A.mult))
+    V(v.tensor_scalar(T.cst[:], T.kf[:, 1:2], LIFT - 4.0, T.kf[:, 0:1], A.mult, A.add))
     need("v", "vec", i_m)
     V(v.tensor_scalar(T.dmk[:], T.dmb[:], -FAR, None, A.add))
-    need("v", "vec", i_c)
-    V(v.tensor_scalar(T.cst[:], T.csu[:], T.kf[:, 1:2], -4.0, A.add, A.add))
-    V(v.memset(T.g2[:], 0.0))
-    V(v.memset(T.xs[:, 4 * TOK:], 0.0))
     need("v", "lw", 16)
     i_w = V(v.quantize_mx(T.wc[:, 0:128], T.wp[:, 0:128], T.ws[:]))
+
+    def quant_x(h):
+        need("v", "lx%d" % h, 16)
+        return V(v.quantize_mx(T.xc[:, HX * h:HX * h + HX], T.xp[:, HX * h:HX * h + HX], T.xs[:, 4 * HX * h:4 * HX * (h + 1)]))
+
+    i_x = quant_x(0)
+    need("s", "vec", i_k)
+    need("s", "gc", i_tab)
+    i_st = S(sc.activation(T.stt[:], T.tab[:, 0:64].indirect(T.pou[:, 0:4]), F.Copy, bias=LOW, scale=4.0))
     need("v", "gc", i_tab)
-    i_ln = V(v.tensor_copy(T.lnt[:], T.tab[:, 64:128].indirect(T.pou[:, 0:4])))
-    i_st = V(v.tensor_scalar(T.stt[:], T.tab[:, 0:64].indirect(T.pou[:, 0:4]), 4.0, None, A.mult))
-    need("v", "vec", i_ln)
-    i = V(v.tensor_scalar(T.nes[:], T.lnt[:], -4.0, None, A.mult))
+    i = V(v.tensor_scalar(T.lnt[:], T.tab[:, 64:128].indirect(T.pou[:, 0:4]), 4.0, None, A.mult))
+    need("v", "act", i_st)
     need("v", "vec", i)
-    i_ne = V(v.tensor_tensor(T.nen[:], T.nes[:], T.stt[:], A.subtract))
-    need("v", "lx", 16)
-    i_x = V(v.quantize_mx(T.xc[:], T.xp[:], T.xs[:, 0:4 * TOK]))
+    i_ne = V(v.tensor_tensor(T.ent[:], T.lnt[:], T.stt[:], A.add))
+
+    def x_half(h, i):
+        need("g", "vec", i)
+        for ap in (u8(T.xc[:, HX * h:HX * h + HX]), T.xp[:, HX * h:HX * h + HX]):
+            fused([(hs[2], ap, ap, "hx%d" % h, half(topo, core, hs[2], 1) if h else topo.engines(core, hs[2]))])
 
     need("g", "vec", i_w)
     fused([(hs[n], u8(T.wc[:, 0:128]), u8(T.wc[:, 0:128]), "hw", half(topo, core, hs[n], n)) for n in range(2)])
-    fused([(hs[n], T.wp[:, 0:128], T.wp[:, 0:128], "hv", half(topo, core, hs[n], n)) for n in range(2)])
-    need("g", "vec", i_x)
-    fused([(hs[2], u8(T.xc[:]), u8(T.xc[:]), "hx", topo.engines(core, hs[2]))])
-    fused([(hs[2], T.xp[:], T.xp[:], "hx", topo.engines(core, hs[2]))])
+    fused([(hs[3], T.wp[:, 0:128], T.wp[:, 0:128], "hv", topo.engines(core, hs[3]))])
+    x_half(0, i_x)
 
     def ends(bt, R, off, on_s, fill=None):
         gb, eb, vb = GB[bt], EB[bt], VB[bt]
         w = 16 * R
-        need("v", "vec", i_ne)
         if on_s:
-            need("s", "vec", i_st)
+            need("s", "act", i_st)
             st = ("act", S(sc.activation(T.g2[:, gb:gb + w], T.stt[:, 0:64].indirect(off), F.Copy)))
         i = V(v.tensor_tensor(T.g1[:, gb:gb + w], T.lnt[:, 0:64].indirect(off), T.le[:, 0:w], A.mult))
         if not on_s:
@@ -336,7 +369,8 @@ def rank_program(g, core, T, topo):
         need("v", "vec", i)
         i_n = V(v.tensor_tensor_scan(T.s1[:, gb:gb + w], T.rst[:, 0:w], T.g1[:, gb:gb + w], 0.0, A.max, A.add))
         need("v", *st)
-        i_d = V(v.tensor_tensor(T.dl[:, gb:gb + w], T.nen[:, 0:64].indirect(off), T.g2[:, gb + 1:gb + w + 1], A.add))
+        need("v", "vec", i_ne)
+        i_d = V(v.tensor_tensor(T.dl[:, gb:gb + w], T.ent[:, 0:64].indirect(off), T.g2[:, gb + 1:gb + w + 1], A.subtract))
         need("v", "vec", i_n)
         i_e = V(v.tensor_copy(T.en0[:, eb:eb + R], T.s1[:, gb + 15:gb + w:16]))
         need("v", "vec", max(i_d, i_e))
@@ -350,7 +384,7 @@ def rank_program(g, core, T, topo):
         for b in bs:
             p, c = 128 * (PB[bt] + b), VB[bt] + WB * b
             i1.append(V(v.tensor_tensor_scan(T.la[:, p:p + 128], T.fr[:], T.vv[:, c:c + 128],
-                                             T.g2[:, GB[bt] + 16 * b:GB[bt] + 16 * b + 1], A.add, A.add)))
+                                             T.g2[:, GB[bt] + 16 * b:GB[bt] + 16 * b + 1], A.add, A.subtract)))
         for b, i in zip(bs, i1):
             p = 128 * (PB[bt] + b)
             need("v", "vec", i)
@@ -358,13 +392,13 @@ def rank_program(g, core, T, topo):
         t, n = PB[bt] + bs[0], len(bs)
         x = fill and fill()
         need("v", "vec", i2)
-        return V(v.tensor_scalar(T.off[:, 32 * t:32 * (t + n)], T.lb[:, 128 * t + 3:128 * (t + n):4], T.cst[:], None, A.add)), x
+        return V(v.tensor_scalar(T.off[:, 32 * t:32 * (t + n)], T.lb[:, 128 * t + 3:128 * (t + n):4], T.cst[:],
+                                 4.0 * TOK - 1.0, A.add, A.min)), x
 
     def win(t):
         return T.xs[:, :].indirect(T.off[:, 32 * t:32 * t + 32])
 
     def gather_s(t, i):
-        need("s", "lx", 16)
         need("s", "vec", i)
         return S(sc.activation(T.tile[:, 512 * t:512 * t + 512], win(t), F.Copy))
 
@@ -394,53 +428,69 @@ def rank_program(g, core, T, topo):
 
     need("v", "cds", n_same)
     need("s", "cds", n_same)
-    _, s_s, _ = ends("S", 3, T.cds[:, 0:3], True)
+    _, s_s, i_x = ends("S", 3, T.cds[:, 0:3], True, lambda: quant_x(1))
+    x_half(1, i_x)
+    S(sc.activation(T.neg[:], T.zz[:, 0:64], F.Copy, bias=-BIG))
+    S(sc.activation(T.mko[:], T.zz[:, 0:WX], F.Copy, bias=BIG))
+    i_mk = S(sc.activation(T.mk[:], T.zz[:, 0:680], F.Copy, bias=BIG))
     i0 = gather_s(0, offsets("S", [0], s_s)[0])
-    i1 = gather_s(1, offsets("S", [1], s_s)[0])
+    o_s, _ = offsets("S", [1, 2], s_s)
+    i1 = gather_s(1, o_s)
 
     need("v", "cdo", 2 * n_off)
     i_e, s_o, i_q = ends("O", 2, T.cdo[:, 0:2], False, lambda: quant(0, "act", i0))
     need("g", "vec", i_e)
     fused([(dst(t), T.el[:, t:t + 1], T.en0[:, t:t + 1], "ens", lane(topo, core, dst(t), t)) for t in range(3)]
-          + [(hs[2], T.hen[:, n:n + 1], T.en0[:, EB["O"] + n:EB["O"] + n + 1], "hen", upper(topo, core, hs[2], n))
+          + [(hs[n], T.hen[:], T.en0[:, EB["O"] + n:EB["O"] + n + 1], "hen", upper(topo, core, hs[n], n))
              for n in range(2)])
     need("g", "vec", i_q)
-    codes_across(0)
+    fused([(hs[3], u8(T.hc[:]), codes(0), "hc", half(topo, core, hs[3], 1))])
+    fused([plane_across(0)])
     o, i_q = offsets("O", [0, 1], s_o, lambda: quant(1, "act", i1))
     i3 = gather_s(3, o)
     need("g", "vec", i_q)
     codes_across(1)
+    i2 = gather_s(2, o_s)
+    i_so = S(sc.activation(T.so[:, 0:688], T.zz[:], F.Copy))
     i4 = gather_v(4, o)
-    o, _ = offsets("S", [2], s_s, lambda: quant(3, "act", i3))
-    i2 = gather_s(2, o)
+    quant(3, "act", i3)
     i_q = quant(4, "vec", i4)
     need("g", "vec", i_q)
-    fused([(hs[n], u8(T.hc[:]), codes(3 + n), "hc", half(topo, core, hs[n], n)) for n in range(2)])
-    fused([(hs[2 + n], T.hp[:], plane(3 + n), "hp", upper(topo, core, hs[2 + n], n)) for n in range(2)]
-          + [plane_across(t) for t in range(2)])
+    fused([(hs[k], u8(T.hc[:]), codes(3 + n), "hc", half(topo, core, hs[k], n)) for n, k in enumerate(CODES)])
+    fused([(hs[k], T.hp[:], plane(3 + n), "hp", upper(topo, core, hs[k], n)) for n, k in enumerate(PLANES)]
+          + [plane_across(1)])
 
-    i_l = V(v.tensor_copy(T.cdm[:, 0:1], T.cdu[:, rank:rank + 1]))
-    need("v", "vec", i_l)
-    _, s_m, i_q = ends("M", 1, T.cdm[:, 0:1], False, lambda: quant(2, "act", i2))
-    need("g", "vec", i_q)
+    need("t", "vec", i_x)
+    i_pe = done("pe", pe.matmul_mx(T.ps[:, 512 * 5:512 * 6], T.wc[:, 0:128], T.wp[:, 0:128], T.xc[:], T.xp[:], True, True))
+    V(v.tensor_copy(T.cdm[:, 0:1], T.cdu[:, rank:rank + 1]))
+    i = V(v.tensor_scalar(T.eq[:], T.ii[:, 0:16], T.kf[:, 0:1], 0.25, A.is_equal, A.mult))
+    need("v", "vec", i)
+    for h, tb in enumerate((T.stt, T.ent)):
+        i = V(v.tensor_tensor(T.og[:, 16 * h:16 * h + 16], tb[:, 0:64].indirect(T.cdm[:, 0:1]), T.eq[:], A.mult))
+    need("v", "vec", i)
+    for h in range(2):
+        i = V(v.tensor_reduce(T.of[:, h:h + 1], T.og[:, 16 * h:16 * h + 16], AxisListType.X, A.add))
+    need("g", "vec", quant(2, "act", i2))
     codes_across(2)
     fused([plane_across(2)])
-    i5 = gather_s(5, offsets("M", [0], s_m)[0])
+    need("v", "vec", i)
+    i = V(v.tensor_scalar(T.ou[:, 0:4:2], T.of[:, 0:2], -LOW / 4, None, A.add))
+    need("v", "vec", i)
+    need("v", "act", i_mk)
+    i_bo = V(v.tensor_copy(T.mko[:, 0:WX].indirect(T.ou[:, 0:1]), T.neg[:, 0:16]))
 
-    batch = ["S", "S", "S", "O", "O", "M"]
+    batch = ["S", "S", "S", "O", "O"]
 
     def last(s, n):
         c = EB[batch[s]] + s - PB[batch[s]]
-        return (T.en0 if s == 5 else T.el)[:, c:c + n]
+        return T.el[:, c:c + n]
 
     def border(bt, R):
         return V(v.tensor_copy(T.mk[:, VB[bt]:VB[bt] + WB * R].indirect(last(PB[bt], R)), T.neg[:, 0:16 * R]))
 
-    need("v", "act", i_mk)
     need("v", "ens", n_same)
     border("S", 3)
-    border("M", 1)
-    need("v", "eno", n_off)
+    need("v", "eno", 2 * n_off)
     i_b = border("O", 2)
 
     def tile_engines(s):
@@ -456,32 +506,35 @@ def rank_program(g, core, T, topo):
         for s in slots:
             c = VB[bt] + WB * (s - PB[bt])
             ps = T.ps[:, 512 * s:512 * s + 128]
-            need("t", "vec", i_w)
-            if s == 5:
-                need("t", "vec", i_own)
-                i = done("pe", pe.matmul_mx(ps, T.wc[:, 0:128], T.wp[:, 0:128], T.qc[:, 640:768], T.qp[:, 640:768], True, True))
-            else:
-                need("t", "t%d" % s, tile_engines(s))
-                i = done("pe", pe.matmul_mx(ps, T.wc[:, 0:128], T.wp[:, 0:128], T.lc[:, 128 * s:128 * s + 128],
-                                            T.lp[:, 128 * s:128 * s + 128], True, True))
+            need("t", "t%d" % s, tile_engines(s))
+            i = done("pe", pe.matmul_mx(ps, T.wc[:, 0:128], T.wp[:, 0:128], T.lc[:, 128 * s:128 * s + 128],
+                                        T.lp[:, 128 * s:128 * s + 128], True, True))
             need("v", "pe", i)
             need("v", "vec", i_b)
             i = V(v.tensor_tensor_scan(T.so[:, c + 1:c + 129], T.mk[:, c:c + 128], ps, -BIG, A.min, A.max))
         need("s", "vec", i)
         s, n = slots[0], len(slots)
         i = S(sc.activation(T.ys[:, 16 * s:16 * (s + n)], T.so[:, VB[bt]:c + WB].indirect(last(s, n)), F.Copy))
-        need("y", "act", i)
         for s in slots:
-            store(rank if s == 5 else src(s) if s < 3 else til[s - 3], T.ys[:, 16 * s:16 * s + 16])
+            on = "s" if s == 4 else "y"
+            need(on, "act", i)
+            store(src(s) if s < 3 else til[s - 3], T.ys[:, 16 * s:16 * s + 16], on)
 
-    i_own = quant(5, "act", i5)
-    score((5,))
+    need("v", "pe", i_pe)
+    need("v", "act", i_so)
+    need("v", "vec", i_bo)
+    c = VB["M"]
+    i = V(v.tensor_tensor_scan(T.so[:, c + 1:c + 1 + TOK], T.mko[:, 0:TOK], T.ps[:, 512 * 5:512 * 6], -BIG, A.min, A.max))
+    need("s", "vec", i)
+    i = S(sc.activation(T.ys[:, 80:96], T.so[:, c:c + 1 + TOK].indirect(T.ou[:, 2:3]), F.Copy))
+    need("y", "act", i)
+    store(rank, T.ys[:, 80:96])
     score((0, 1))
     for m in range(2):
         need("y", "r%d" % m, n_off // 2)
         store(sco[m], T.yr[:, 16 * m:16 * m + 16])
-    score((3, 4))
     score((2,))
+    score((3, 4))
 
     for sem in cnt:
         need("g", sem, cnt[sem])

from concourse.bass import DstId, RemoteDMATransfer
from concourse.mybir import dt, AluOpType as A, ActivationFunctionType as F, AxisListType

N, ND, TOK = 8, 64, 512
HX = TOK // 2
BIG, FAR, LIFT = 1.0e29, 1.0e6, 4096.0
LOW = -3.0 * LIFT - 4.0
WB = 136
WX = 520
VB = {"S": 0, "O": 408, "M": 680}
GB = {"S": 0, "O": 56, "M": 96}
EB = {"S": 0, "O": 4, "M": 8}
PB = {"S": 0, "O": 3, "M": 5}
CODES, PLANES = (0, 1), (2, 3)

SCRATCH = {
    "cdi": ("sbuf", [128, 8], "int32"), "cdu": ("sbuf", [128, 8], "uint16"), "cdf": ("sbuf", [128, 8], "float32"),
    "cdm": ("sbuf", [128, 2], "uint16"), "tci": ("sbuf", [128, 1], "int32"), "pk": ("sbuf", [128, 2], "uint16"),
    "row": ("sbuf", [1, 128], "int32"), "rowf": ("sbuf", [1, 128], "float32"), "tab": ("sbuf", [128, 128], "float32"),
    "stt": ("sbuf", [128, 64], "float32"), "lnt": ("sbuf", [128, 64], "float32"),
    "ent": ("sbuf", [128, 64], "float32"),
    "poi": ("sbuf", [128, 4], "int32"), "poa": ("sbuf", [128, 4], "int32"), "pou": ("sbuf", [128, 4], "uint16"),
    "ki": ("sbuf", [128, 2], "int32"), "kf": ("sbuf", [128, 2], "float32"),
    "cst": ("sbuf", [128, 1], "float32"), "zz": ("sbuf", [128, 688], "bfloat16"),
    "ii": ("sbuf", [128, 48], "float32"), "jj": ("sbuf", [128, 128], "float32"),
    "le": ("sbuf", [128, 48], "float32"), "dmb": ("sbuf", [128, 128], "float32"), "dmk": ("sbuf", [128, 128], "float32"),
    "rst": ("sbuf", [128, 48], "float32"), "fr": ("sbuf", [128, 128], "float32"), "neg": ("sbuf", [128, 64], "float32"),
    "cds": ("sbuf", [128, 4], "uint16"), "cdo": ("sbuf", [128, 2], "uint16"),
    "g1": ("sbuf", [128, 120], "float32"), "s1": ("sbuf", [128, 120], "float32"), "g2": ("sbuf", [128, 120], "float32"),
    "dl": ("sbuf", [128, 120], "float32"), "en0": ("sbuf", [128, 16], "uint16"),
    "vv": ("sbuf", [128, 680], "float32"),
    "la": ("sbuf", [128, 640], "float32"), "lb": ("sbuf", [128, 640], "float32"),
    "off": ("sbuf", [128, 160], "uint16"),
    "xs": ("sbuf", [128, 4 * TOK], "bfloat16"), "ws": ("sbuf", [128, 512], "bfloat16"),
    "tile": ("sbuf", [128, 3072], "bfloat16"),
    "qc": ("sbuf", [128, 768], "float8_e4m3fn_x4"), "qp": ("sbuf", [128, 768], "uint8"),
    "xc": ("sbuf", [128, 512], "float8_e4m3fn_x4"), "xp": ("sbuf", [128, 512], "uint8"),
    "wc": ("sbuf", [128, 256], "float8_e4m3fn_x4"), "wp": ("sbuf", [128, 256], "uint8"),
    "lc": ("sbuf", [128, 640], "float8_e4m3fn_x4"), "lp": ("sbuf", [128, 640], "uint8"),
    "el": ("sbuf", [128, 8], "uint16"), "yr": ("sbuf", [128, 32], "float32"),
    "eq": ("sbuf", [128, 16], "float32"), "og": ("sbuf", [128, 64], "float32"), "of": ("sbuf", [128, 4], "float32"),
    "ou": ("sbuf", [128, 8], "uint16"), "mko": ("sbuf", [128, WX], "float32"),
    "mk": ("sbuf", [128, 680], "float32"), "so": ("sbuf", [128, 680 + WX], "float32"), "ys": ("sbuf", [128, 96], "float32"),
    "ps": ("psum", [128, 3072], "float32"),
    "hcd": ("sbuf", [128, 1], "uint16"), "hen": ("sbuf", [128, 1], "uint16"),
    "hc": ("sbuf", [128, 128], "float8_e4m3fn_x4"), "hp": ("sbuf", [128, 128], "uint8"),
    "htd": ("dram", [128, 1], "uint16"),
    "hl": ("sbuf", [128, 2], "uint16"), "hli": ("sbuf", [128, 2], "int32"), "hlj": ("sbuf", [128, 4], "int32"),
    "hlf": ("sbuf", [128, 4], "float32"), "hlu": ("sbuf", [128, 4], "uint16"), "hrow": ("sbuf", [1, 128], "uint16"),
}
SEMAPHORES = (["vec", "act", "pe", "gc", "lcd", "ltab", "ltc", "lx0", "lx1", "lw", "ly", "sent", "cds", "cdo", "ens", "eno",
               "hcd", "htb", "hen", "hc", "hp", "hw", "hv", "hx0", "hx1", "hl", "hq0", "hq1", "r0", "r1"] + ["t%d" % s for s in range(5)])


def groups(T, topo, r):
    def halves(u):
        own = [q for q in range(N) if q == u or topo.may_write(T.cores[u], T.cores[q])]
        oth = [q for q in range(N) if q not in own]
        a = own.index(u)
        rot = [oth[(a + k) % len(oth)] for k in range(len(oth))]
        return [own[(a + j) % len(own)] for j in range(len(own))], rot[0::2], rot[1::2]

    def mated(i):
        return sum(topo.mates(T.cores[u], T.cores[q]) for u in range(N) for q in halves(u)[i])

    own, ev, od = halves(r)
    return (own, ev, od) if mated(1) >= mated(2) else (own, od, ev)


def helpers(T, topo, r):
    c = T.cores[r]
    dst = T.cores[groups(T, topo, r)[1][0]]
    hs = [h for h in topo.cores_of(c) if h != c and topo.may_write(h, dst)]
    near = [h for h in hs if topo.die(h) == topo.die(c)]
    far = [h for h in hs if topo.die(h) != topo.die(c)]
    return [near[0], far[0], near[1], far[1]]


def part(e, i, n):
    w = len(e) // n
    return e[i * w:(i + 1) * w]


def bits(e):
    return sum(1 << x for x in e)


def upper(topo, c, h, k, n=2):
    return part(part(topo.engines(c, h), 1, 2), k, n)


def half(topo, c, h, k):
    return part(topo.engines(c, h), k, 2)


def lane(topo, c, d, t):
    return part(topo.engines(c, d), t, 4)


def plane_same(topo, c, d, t):
    return topo.engines(c, d)


def u8(ap):
    return ap.bitcast(dt.uint8)


def caller(g, core, T, topo):
    queue = {"v": g.vector, "s": g.scalar, "t": g.tensor, "g": g, "y": g.sync}
    cnt = {"vec": 0, "act": 0, "pe": 0, "gc": 0, "sent": 0}
    seen = {}

    def need(q, sem, val):
        if seen.get((q, sem), 0) < val:
            queue[q].wait_ge(T.sem[sem], int(val))
            seen[(q, sem)] = val

    def done(sem, ins):
        cnt[sem] += 1
        ins.then_inc(T.sem[sem], 1)
        return cnt[sem]

    def fused(trs):
        ts = []
        for dc, dst, src, sem, e in trs:
            rid, pid = topo.addr(dc, core)
            ts.append(RemoteDMATransfer(dst_ids=[DstId(rid=rid, pnc=pid)], dma_engine_mask=bits(e),
                                        remote_sem=T.sem[sem], src=src, dst=dst))
            cnt["sent"] += len(e)
        g.remote_dma_fused(ts, local_sem=T.sem.sent)

    return need, done, fused, cnt


def score_all(g, T, need, done, i_io, n_tab, n_list, n_x, n_w):
    v, sc, pe = g.vector, g.scalar, g.tensor

    def V(ins):
        return done("vec", ins)

    mk = (T.mk, T.mko)
    for n in range(2):
        V(v.memset(mk[n][:, 0:WX], BIG))
    V(v.memset(T.neg[:], -BIG))
    V(v.memset(T.so[:, 0:2 * WX], 0.0))
    need("v", "gc", i_io)
    i = V(v.tensor_scalar(T.ki[:, 0:1], T.poi[:, 0:1], 15, None, A.bitwise_and))
    need("v", "vec", i)
    i = V(v.tensor_copy(T.kf[:, 0:1], T.ki[:, 0:1]))
    need("v", "vec", i)
    V(v.tensor_scalar(T.eq[:], T.ii[:, 0:16], T.kf[:, 0:1], None, A.is_equal))
    need("y", "htb", n_tab)
    g.sync.dma_start(T.hrow[0:1, :], T.htd[:]).then_inc(T.sem.ltab, 16)
    need("v", "ltab", 16)
    i = V(v.tensor_copy(T.rowf[0:1, :], T.hrow[0:1, :]))
    need("v", "vec", i)
    need("g", "vec", V(v.tensor_tensor(T.rowf[0:1, 64:128], T.rowf[0:1, 64:128], T.rowf[0:1, 0:64], A.add)))
    i_tab = done("gc", g.partition_broadcast(T.tab[:], T.rowf[0:1, :], 128))
    need("v", "hl", n_list)
    i = V(v.tensor_copy(T.hli[:], T.hl[:]))
    need("v", "vec", i)
    for n, low in enumerate((6, 0)):
        V(v.tensor_scalar(T.hlj[:, n:n + 1], T.hli[:, n:n + 1], low, 15, A.logical_shift_right, A.bitwise_and))
        i = V(v.tensor_scalar(T.hlj[:, 2 + n:3 + n], T.hli[:, n:n + 1], low + 4, 3, A.logical_shift_right, A.bitwise_and))
    need("v", "vec", i)
    i = V(v.tensor_copy(T.hlf[:], T.hlj[:]))
    need("v", "vec", i)
    for n in range(2):
        i = V(v.tensor_scalar(T.hlu[:, 2 * n:2 * n + 1], T.hlf[:, n:n + 1], 4.0, T.hlf[:, 2 + n:3 + n], A.mult, A.add))
    need("v", "vec", i)
    need("v", "gc", i_tab)
    for j in range(4):
        i = V(v.tensor_tensor(T.og[:, 16 * j:16 * j + 16], T.tab[:, 64 * (j % 2):64 * (j % 2) + 64].indirect(
            T.hlu[:, 2 * (j // 2):2 * (j // 2) + 1]), T.eq[:], A.mult))
    need("v", "vec", i)
    for j in range(4):
        i = V(v.tensor_reduce(T.of[:, j:j + 1], T.og[:, 16 * j:16 * j + 16], AxisListType.X, A.add))
    need("v", "vec", i)
    i = V(v.tensor_copy(T.ou[:, 0:8:2], T.of[:]))
    need("v", "vec", i)
    for n in range(2):
        i_l = V(v.tensor_copy(mk[n][:, 0:WX].indirect(T.ou[:, 4 * n:4 * n + 1]), T.neg[:, 0:16]))
    i_s = [i_l, i_l]
    for h, n in ((0, 0), (0, 1), (1, 0), (1, 1)):
        need("t", "hx%d" % h, n_x // (1 + h))
        need("t", "hq%d" % n, n_w)
        ps = T.ps[:, 512 * (2 * h + n):512 * (2 * h + n) + HX]
        i = done("pe", pe.matmul_mx(ps, T.wc[:, 128 * n:128 * n + 128], T.wp[:, 128 * n:128 * n + 128],
                                    T.xc[:, HX * h:HX * h + HX], T.xp[:, HX * h:HX * h + HX], True, True))
        need("v", "vec", i_s[n])
        need("v", "pe", i)
        c = WX * n + HX * h
        i_s[n] = V(v.tensor_tensor_scan(T.so[:, c + 1:c + 1 + HX], mk[n][:, HX * h:HX * h + HX], ps,
                                        T.so[:, c:c + 1] if h else -BIG, A.min, A.max))
    for n in range(2):
        need("s", "vec", i_s[n])
        i = done("act", sc.activation(T.yr[:, 16 * n:16 * n + 16],
                                      T.so[:, WX * n:WX * n + WX].indirect(T.ou[:, 4 * n + 2:4 * n + 3]), F.Copy))
    return i


def hand_on(g, core, T, topo, r, k):
    own, til, sco = groups(T, topo, r)
    rc = T.cores[r]
    need, done, fused, cnt = caller(g, core, T, topo)
    n = k % 2
    to = T.cores[til[n]]
    e = topo.engines(core, to)
    n_up = len(upper(topo, rc, core, 0))
    n_half = len(half(topo, rc, core, 0))

    def back(m):
        return groups(T, topo, sco[m])[2].index(r)

    def scorer(m):
        return helpers(T, topo, sco[m])[2]

    if k < 2:
        need("g", "hcd", n_up)
        fused([(to, T.cdo[:, n:n + 1], T.hcd[:, 0:1], "cdo", e)])
        b = back(k)
        need("g", "hw", n_half)
        fused([(scorer(k), u8(T.wc[:, 128 * b:128 * b + 128]), u8(T.wc[:, 0:128]), "hq%d" % b, e)])
        need("g", "hen", n_up)
        fused([(to, T.el[:, EB["O"] + n:EB["O"] + n + 1], T.hen[:], "eno", e)])
    elif k == 2:
        done("gc", g.iota(T.poi[:, 0:1], [[0, 1]], 0, 1))
        i_io = done("gc", g.iota(T.ii[:, 0:16], [[1, 16]], 0, 0, allow_small_or_imprecise_dtypes=True))
        need("g", "hcd", n_up)
        fused([(scorer(m), T.hl[:, back(m):back(m) + 1], T.hcd[:, 0:1], "hl", part(e, m, 2)) for m in range(2)])
        i_y = score_all(g, T, need, done, i_io, n_up, len(e), 4 * n_half, len(e) + len(e) // 2)
    else:
        need("g", "hv", 2 * n_half)
        fused([(scorer(m), T.wp[:, 128 * back(m):128 * back(m) + 128], T.wp[:, 0:128], "hq%d" % back(m), part(e, m, 2))
               for m in range(2)])
        need("g", "hc", n_half)
        fused([(T.cores[own[1]], u8(T.lc[:, 0:128]), u8(T.hc[:]), "t0", e)])
    if k in CODES:
        n = CODES.index(k)
        need("g", "hc", n_half)
        fused([(T.cores[til[n]], u8(T.lc[:, 128 * (3 + n):128 * (4 + n)]), u8(T.hc[:]), "t%d" % (3 + n), e)])
    if k in PLANES:
        n = PLANES.index(k)
        need("g", "hp", n_up)
        fused([(T.cores[til[n]], T.lp[:, 128 * (3 + n):128 * (4 + n)], T.hp[:], "t%d" % (3 + n), e)])
    if k == 2:
        need("g", "act", i_y)
        fused([(T.cores[sco[m]], T.yr[:, 16 * back(m):16 * back(m) + 16], T.yr[:, 16 * m:16 * m + 16], "r%d" % back(m),
                part(e, m, 2)) for m in range(2)])
    for sem in cnt:
        need("g", sem, cnt[sem])


def rank_program(g, core, T, topo):
    rank = T.rank_of(core)
    if rank is None:
        for r in range(N):
            if T.cores[r] in topo.cores_of(core):
                hs = helpers(T, topo, r)
                if core in hs:
                    hand_on(g, core, T, topo, r, hs.index(core))
        return
    own, til, sco = groups(T, topo, rank)
    hs = helpers(T, topo, rank)
    v, sc, pe = g.vector, g.scalar, g.tensor
    need, done, fused, cnt = caller(g, core, T, topo)

    def V(ins):
        return done("vec", ins)

    def S(ins):
        return done("act", ins)

    def dst(t):
        return T.cores[own[t + 1]]

    def src(t):
        return own[3 - t]

    for i in range(8):
        (g.sync if i % 2 == 0 else sc).dma_start(T.cdi[16 * i:16 * i + 16, :], T.cd[:]).then_inc(T.sem.lcd, 16)
    g.sync.dma_start(T.row[0:1, 0:64], T.st[:]).then_inc(T.sem.ltab, 16)
    sc.dma_start(T.row[0:1, 64:128], T.ln[:]).then_inc(T.sem.ltab, 16)
    g.sync.dma_start(T.tci[0:64, :], T.st[:]).then_inc(T.sem.ltc, 16)
    sc.dma_start(T.tci[64:128, :], T.ln[:]).then_inc(T.sem.ltc, 16)
    sc.dma_start(T.ws[:], T.qw[:]).then_inc(T.sem.lw, 16)
    for h in range(2):
        g.sync.dma_start(T.xs[:, 4 * HX * h:4 * HX * (h + 1)], T.x[:, 4 * HX * h:4 * HX * (h + 1)]).then_inc(T.sem["lx%d" % h], 16)

    i_io = done("gc", g.iota(T.poi[:], [[1, 4]], 0, 4))
    done("gc", g.iota(T.ii[:], [[0, 3], [1, 16]], 0, 0, allow_small_or_imprecise_dtypes=True))
    done("gc", g.iota(T.jj[:], [[0, 32], [1, 4]], 0, 0, allow_small_or_imprecise_dtypes=True))
    i_ij = done("gc", g.iota(T.rst[:], [[WB, 3], [0, 16]], 0, 0, allow_small_or_imprecise_dtypes=True))

    i_z = V(v.memset(T.zz[:], 0.0))
    need("s", "vec", i_z)
    i_vv = S(sc.activation(T.vv[:], T.zz[:, 0:680], F.Copy))
    i_fr = S(sc.activation(T.fr[:], T.zz[:, 0:128], F.Copy, bias=4.0))
    V(v.memset(T.g2[:], LOW))
    need("v", "gc", i_io)
    V(v.tensor_scalar(T.ki[:, 0:1], T.poi[:, 0:1], 63, 2, A.bitwise_and, A.arith_shift_right))
    V(v.tensor_scalar(T.ki[:, 1:2], T.poi[:, 0:1], 63, 4, A.bitwise_and, A.arith_shift_right))
    i_p = V(v.tensor_scalar(T.poa[:], T.poi[:], 63, None, A.bitwise_and))
    need("v", "vec", i_p)
    V(v.tensor_copy(T.kf[:], T.ki[:]))
    i_k = V(v.tensor_copy(T.pou[:], T.poa[:]))

    need("v", "lcd", 128)
    i_cd = V(v.tensor_copy(T.cdu[:], T.cdi[:]))
    i = V(v.tensor_copy(T.cdf[:], T.cdi[:]))
    need("v", "ltab", 32)
    i_row = V(v.tensor_copy(T.rowf[0:1, :], T.row[0:1, :]))
    need("v", "ltc", 32)
    V(v.tensor_copy(T.pk[:, 1:2], T.tci[:]))
    need("v", "vec", i)
    i_pk = V(v.tensor_scalar(T.pk[:, 0:1], T.cdf[:, sco[1]:sco[1] + 1], float(ND), T.cdf[:, sco[0]:sco[0] + 1], A.mult, A.add))
    need("g", "vec", i_cd)
    fused([(T.cores[src(t)], T.cds[:, t:t + 1], T.cdu[:, src(t):src(t) + 1], "cds", lane(topo, core, T.cores[src(t)], t))
           for t in range(3)]
          + [(hs[n], T.hcd[:, 0:1], T.cdu[:, til[n]:til[n] + 1], "hcd", upper(topo, core, hs[n], n)) for n in range(2)])
    need("g", "vec", i_row)
    i_tab = done("gc", g.partition_broadcast(T.tab[:], T.rowf[0:1, :], 128))
    need("g", "vec", i_pk)
    fused([(hs[2], (T.hcd, T.htd)[n][:], T.pk[:, n:n + 1], ("hcd", "htb")[n], upper(topo, core, hs[2], n)) for n in range(2)])

    need("v", "gc", i_ij)
    need("v", "vec", i_k)
    i_m = V(v.tensor_scalar(T.dmb[:], T.jj[:], T.kf[:, 1:2], FAR + LIFT, A.is_gt, A.mult))
    V(v.tensor_scalar(T.le[:], T.ii[:], T.kf[:, 0:1], 0.25, A.is_le, A.mult))
    V(v.tensor_scalar(T.cst[:], T.kf[:, 1:2], LIFT - 4.0, T.kf[:, 0:1], A.mult, A.add))
    need("v", "vec", i_m)
    V(v.tensor_scalar(T.dmk[:], T.dmb[:], -FAR, None, A.add))
    need("v", "lw", 16)
    i_w = V(v.quantize_mx(T.wc[:, 0:128], T.wp[:, 0:128], T.ws[:]))

    def quant_x(h):
        need("v", "lx%d" % h, 16)
        return V(v.quantize_mx(T.xc[:, HX * h:HX * h + HX], T.xp[:, HX * h:HX * h + HX], T.xs[:, 4 * HX * h:4 * HX * (h + 1)]))

    i_x = quant_x(0)
    need("s", "vec", i_k)
    need("s", "gc", i_tab)
    i_st = S(sc.activation(T.stt[:], T.tab[:, 0:64].indirect(T.pou[:, 0:4]), F.Copy, bias=LOW, scale=4.0))
    need("v", "gc", i_tab)
    i = V(v.tensor_scalar(T.lnt[:], T.tab[:, 64:128].indirect(T.pou[:, 0:4]), 4.0, None, A.mult))
    need("v", "act", i_st)
    need("v", "vec", i)
    i_ne = V(v.tensor_tensor(T.ent[:], T.lnt[:], T.stt[:], A.add))

    def x_half(h, i):
        need("g", "vec", i)
        for ap in (u8(T.xc[:, HX * h:HX * h + HX]), T.xp[:, HX * h:HX * h + HX]):
            fused([(hs[2], ap, ap, "hx%d" % h, half(topo, core, hs[2], 1) if h else topo.engines(core, hs[2]))])

    need("g", "vec", i_w)
    fused([(hs[n], u8(T.wc[:, 0:128]), u8(T.wc[:, 0:128]), "hw", half(topo, core, hs[n], n)) for n in range(2)])
    fused([(hs[3], T.wp[:, 0:128], T.wp[:, 0:128], "hv", topo.engines(core, hs[3]))])
    x_half(0, i_x)

    def ends(bt, R, off, on_s, fill=None):
        gb, eb, vb = GB[bt], EB[bt], VB[bt]
        w = 16 * R
        if on_s:
            need("s", "act", i_st)
            st = ("act", S(sc.activation(T.g2[:, gb:gb + w], T.stt[:, 0:64].indirect(off), F.Copy)))
        i = V(v.tensor_tensor(T.g1[:, gb:gb + w], T.lnt[:, 0:64].indirect(off), T.le[:, 0:w], A.mult))
        if not on_s:
            st = ("vec", V(v.tensor_copy(T.g2[:, gb:gb + w], T.stt[:, 0:64].indirect(off))))
        need("v", "vec", i)
        i_n = V(v.tensor_tensor_scan(T.s1[:, gb:gb + w], T.rst[:, 0:w], T.g1[:, gb:gb + w], 0.0, A.max, A.add))
        need("v", *st)
        need("v", "vec", i_ne)
        i_d = V(v.tensor_tensor(T.dl[:, gb:gb + w], T.ent[:, 0:64].indirect(off), T.g2[:, gb + 1:gb + w + 1], A.subtract))
        need("v", "vec", i_n)
        i_e = V(v.tensor_copy(T.en0[:, eb:eb + R], T.s1[:, gb + 15:gb + w:16]))
        need("v", "vec", max(i_d, i_e))
        need("v", "act", max(i_vv, i_fr))
        i_s = V(v.tensor_copy(T.vv[:, vb:vb + WB * R].indirect(T.en0[:, eb:eb + R]), T.dl[:, gb:gb + w]))
        return i_e, i_s, fill and fill()

    def offsets(bt, bs, i_s, fill=None):
        need("v", "vec", i_s)
        i1 = []
        for b in bs:
            p, c = 128 * (PB[bt] + b), VB[bt] + WB * b
            i1.append(V(v.tensor_tensor_scan(T.la[:, p:p + 128], T.fr[:], T.vv[:, c:c + 128],
                                             T.g2[:, GB[bt] + 16 * b:GB[bt] + 16 * b + 1], A.add, A.subtract)))
        for b, i in zip(bs, i1):
            p = 128 * (PB[bt] + b)
            need("v", "vec", i)
            i2 = V(v.tensor_tensor_scan(T.lb[:, p:p + 128], T.dmk[:], T.la[:, p:p + 128], 0.0, A.add, A.max))
        t, n = PB[bt] + bs[0], len(bs)
        x = fill and fill()
        need("v", "vec", i2)
        return V(v.tensor_scalar(T.off[:, 32 * t:32 * (t + n)], T.lb[:, 128 * t + 3:128 * (t + n):4], T.cst[:],
                                 4.0 * TOK - 1.0, A.add, A.min)), x

    def win(t):
        return T.xs[:, :].indirect(T.off[:, 32 * t:32 * t + 32])

    def gather_s(t, i):
        need("s", "vec", i)
        return S(sc.activation(T.tile[:, 512 * t:512 * t + 512], win(t), F.Copy))

    def gather_v(t, i):
        need("v", "vec", i)
        return V(v.tensor_copy(T.tile[:, 512 * t:512 * t + 512], win(t)))

    def quant(t, sem, i):
        need("v", sem, i)
        return V(v.quantize_mx(T.qc[:, 128 * t:128 * t + 128], T.qp[:, 128 * t:128 * t + 128],
                               T.tile[:, 512 * t:512 * t + 512]))

    def codes(t):
        return u8(T.qc[:, 128 * t:128 * t + 128])

    def plane(t):
        return T.qp[:, 128 * t:128 * t + 128]

    def codes_across(t):
        fused([(dst(t), u8(T.lc[:, 128 * t:128 * t + 128]), codes(t), "t%d" % t, topo.engines(core, dst(t)))])

    def plane_across(t):
        return dst(t), T.lp[:, 128 * t:128 * t + 128], plane(t), "t%d" % t, plane_same(topo, core, dst(t), t)

    n_off = len(topo.engines(hs[0], T.cores[til[0]]))
    n_same = sum(len(lane(topo, T.cores[src(t)], core, t)) for t in range(3))

    need("v", "cds", n_same)
    need("s", "cds", n_same)
    _, s_s, i_x = ends("S", 3, T.cds[:, 0:3], True, lambda: quant_x(1))
    x_half(1, i_x)
    S(sc.activation(T.neg[:], T.zz[:, 0:64], F.Copy, bias=-BIG))
    S(sc.activation(T.mko[:], T.zz[:, 0:WX], F.Copy, bias=BIG))
    i_mk = S(sc.activation(T.mk[:], T.zz[:, 0:680], F.Copy, bias=BIG))
    i0 = gather_s(0, offsets("S", [0], s_s)[0])
    o_s, _ = offsets("S", [1, 2], s_s)
    i1 = gather_s(1, o_s)

    need("v", "cdo", 2 * n_off)
    i_e, s_o, i_q = ends("O", 2, T.cdo[:, 0:2], False, lambda: quant(0, "act", i0))
    need("g", "vec", i_e)
    fused([(dst(t), T.el[:, t:t + 1], T.en0[:, t:t + 1], "ens", lane(topo, core, dst(t), t)) for t in range(3)]
          + [(hs[n], T.hen[:], T.en0[:, EB["O"] + n:EB["O"] + n + 1], "hen", upper(topo, core, hs[n], n))
             for n in range(2)])
    need("g", "vec", i_q)
    fused([(hs[3], u8(T.hc[:]), codes(0), "hc", half(topo, core, hs[3], 1))])
    fused([plane_across(0)])
    o, i_q = offsets("O", [0, 1], s_o, lambda: quant(1, "act", i1))
    i3 = gather_s(3, o)
    need("g", "vec", i_q)
    codes_across(1)
    i2 = gather_s(2, o_s)
    i_so = S(sc.activation(T.so[:, 0:688], T.zz[:], F.Copy))
    i4 = gather_v(4, o)
    quant(3, "act", i3)
    i_q = quant(4, "vec", i4)
    need("g", "vec", i_q)
    fused([(hs[k], u8(T.hc[:]), codes(3 + n), "hc", half(topo, core, hs[k], n)) for n, k in enumerate(CODES)])
    fused([(hs[k], T.hp[:], plane(3 + n), "hp", upper(topo, core, hs[k], n)) for n, k in enumerate(PLANES)]
          + [plane_across(1)])

    need("t", "vec", i_x)
    i_pe = done("pe", pe.matmul_mx(T.ps[:, 512 * 5:512 * 6], T.wc[:, 0:128], T.wp[:, 0:128], T.xc[:], T.xp[:], True, True))
    V(v.tensor_copy(T.cdm[:, 0:1], T.cdu[:, rank:rank + 1]))
    i = V(v.tensor_scalar(T.eq[:], T.ii[:, 0:16], T.kf[:, 0:1], 0.25, A.is_equal, A.mult))
    need("v", "vec", i)
    for h, tb in enumerate((T.stt, T.ent)):
        i = V(v.tensor_tensor(T.og[:, 16 * h:16 * h + 16], tb[:, 0:64].indirect(T.cdm[:, 0:1]), T.eq[:], A.mult))
    need("v", "vec", i)
    for h in range(2):
        i = V(v.tensor_reduce(T.of[:, h:h + 1], T.og[:, 16 * h:16 * h + 16], AxisListType.X, A.add))
    need("g", "vec", quant(2, "act", i2))
    codes_across(2)
    fused([plane_across(2)])
    need("v", "vec", i)
    i = V(v.tensor_scalar(T.ou[:, 0:4:2], T.of[:, 0:2], -LOW / 4, None, A.add))
    need("v", "vec", i)
    need("v", "act", i_mk)
    i_bo = V(v.tensor_copy(T.mko[:, 0:WX].indirect(T.ou[:, 0:1]), T.neg[:, 0:16]))

    batch = ["S", "S", "S", "O", "O"]

    def last(s, n):
        c = EB[batch[s]] + s - PB[batch[s]]
        return T.el[:, c:c + n]

    def border(bt, R):
        return V(v.tensor_copy(T.mk[:, VB[bt]:VB[bt] + WB * R].indirect(last(PB[bt], R)), T.neg[:, 0:16 * R]))

    need("v", "ens", n_same)
    border("S", 3)
    need("v", "eno", 2 * n_off)
    i_b = border("O", 2)

    def tile_engines(s):
        if s >= 3:
            return 2 * n_off
        return n_off + len(plane_same(topo, T.cores[src(s)], core, s))

    def store(q, ap, on="y"):
        (g.sync if on == "y" else sc).dma_start(T.y[:, 16 * q:16 * q + 16], ap).then_inc(T.sem.ly, 16)

    def score(slots):
        bt = batch[slots[0]]
        for s in slots:
            c = VB[bt] + WB * (s - PB[bt])
            ps = T.ps[:, 512 * s:512 * s + 128]
            need("t", "t%d" % s, tile_engines(s))
            i = done("pe", pe.matmul_mx(ps, T.wc[:, 0:128], T.wp[:, 0:128], T.lc[:, 128 * s:128 * s + 128],
                                        T.lp[:, 128 * s:128 * s + 128], True, True))
            need("v", "pe", i)
            need("v", "vec", i_b)
            i = V(v.tensor_tensor_scan(T.so[:, c + 1:c + 129], T.mk[:, c:c + 128], ps, -BIG, A.min, A.max))
        need("s", "vec", i)
        s, n = slots[0], len(slots)
        i = S(sc.activation(T.ys[:, 16 * s:16 * (s + n)], T.so[:, VB[bt]:c + WB].indirect(last(s, n)), F.Copy))
        for s in slots:
            on = "s" if s == 4 else "y"
            need(on, "act", i)
            store(src(s) if s < 3 else til[s - 3], T.ys[:, 16 * s:16 * s + 16], on)

    need("v", "pe", i_pe)
    need("v", "act", i_so)
    need("v", "vec", i_bo)
    c = VB["M"]
    i = V(v.tensor_tensor_scan(T.so[:, c + 1:c + 1 + TOK], T.mko[:, 0:TOK], T.ps[:, 512 * 5:512 * 6], -BIG, A.min, A.max))
    need("s", "vec", i)
    i = S(sc.activation(T.ys[:, 80:96], T.so[:, c:c + 1 + TOK].indirect(T.ou[:, 2:3]), F.Copy))
    need("y", "act", i)
    store(rank, T.ys[:, 80:96])
    score((0, 1))
    for m in range(2):
        need("y", "r%d" % m, n_off // 2)
        store(sco[m], T.yr[:, 16 * m:16 * m + 16])
    score((2,))
    score((3, 4))

    for sem in cnt:
        need("g", sem, cnt[sem])
    need("g", "ly", 128)
